import numpy as np, ml_dtypes
CORES = [3,11,19,27,35,43,51,59]
N = 8
BF = ml_dtypes.bfloat16
def f(rng, *shape):
    return (rng.standard_normal(shape, dtype=np.float32) * np.exp2(rng.integers(-2, 3, shape[:-1] + (1,)))).astype(BF)
def wide(rng, *shape):
    v = f(rng, *shape).astype(np.float32); k = shape[:-2] + (1, shape[-1])
    return (v * np.exp2(rng.integers(-6, 7, k)) * (rng.random(k) > 0.0625)).astype(BF)
M, K, TR, CAP = 2048, 64, 4, 192
D = 16 * K
def hashes(s, n):
    lo = ((s & 4095) + 1597 * n) & 4095; b = ((s >> 12) + ((lo * lo) >> 6)) & 4095
    return (lo + ((b * b) >> 6)) & 4095, b
def seed_of(a, b, n):
    lo = (a - ((b * b) >> 6)) & 4095
    return ((b - ((lo * lo) >> 6)) & 4095) * 4096 + ((lo - 1597 * n) & 4095)
def owners(t, s):
    a, b = hashes(np.asarray(s, np.int64)[..., None], (TR + 1) * np.arange(K)); w = (a * N) >> 12
    return np.where(b < t[w], w, t[N + w]).astype(np.int64)
def loads(t, s):
    o = owners(t, s); return np.stack([np.sum(o == q, -1) for q in range(N)], -1)
def sixteen(rng, t, keep=()):
    m = 16 - len(keep); kept = np.array(keep, np.int64); base = np.sum(loads(t, kept), 0)
    pool = rng.integers(0, 1 << 24, 1024); c = loads(t, pool); ok = np.flatnonzero(np.all(c * m <= CAP - base, 1)); j = np.arange(m)
    for u in range(m):
        if np.all(np.sum(c[j], 0) + base <= CAP): break
        j[u] = rng.choice(ok)
    return rng.permutation(np.concatenate([pool[j], kept]))
def ranks(rng, least):
    return np.concatenate([rng.integers(least, 4097, N), rng.permutation(N)]).astype(np.int64)
def absent(rng):
    w = rng.permutation(N); t = np.zeros(2 * N, np.int64)
    t[w] = (8192 * np.arange(N) + N - 1) // (2 * (N - 1)); t[N + w] = np.roll(w, -1); return t
def history(rng, dens):
    w = np.zeros((N, 128, M), np.float32)
    for q in range(N):
        for r in range(N):
            w[q] += np.float32(2 ** r) * (rng.random((128, M), dtype=np.float32) < dens[r][:, None])
    return w.astype(BF)
def seeds(rng, rk):
    return np.stack([np.stack([sixteen(rng, rk[g]) for g in range(8)]) for r in range(N)])
def complete(rng, rk, sd, dens=None):
    if dens is None: dens = rng.choice(np.array([0.1, 0.5, 0.9]), (N, 128))
    return {"sd": np.reshape(sd, (N, 128, 1)).astype(np.int32), "rk": np.stack([rk] * N).astype(np.int32), "thr": rng.integers(0, 4097, (N, 8, M)).astype(np.int32),
            "ali": rng.integers(0, M, (N, 8, M)).astype(np.int32), "seen": history(rng, dens), "vec": f(rng, N, 128, M)}
def setup_inputs(rng):
    rk = np.stack([ranks(rng, 2800) for g in range(8)]); return complete(rng, rk, seeds(rng, rk))
def setup_inputs_full(rng):
    o0 = rng.integers(0, N); rk = []
    for g in range(8):
        o = (o0 + g) % N; t = np.concatenate([rng.integers(3874 - 40, 3874 + 41, N), np.full(N, o)]).astype(np.int64); t[o] = 4096; rk.append(t)
    rk = np.stack(rk); sd = seeds(rng, rk); C = CAP // 16
    far = rng.integers(0, N, 8); h = rng.permutation(8); far[h[0]] = 0; far[h[1]] = rng.integers(1, N)
    for g in range(8):
        o = (o0 + g) % N; r = (o + far[g]) % N
        pool = rng.integers(0, 1 << 24, 4096); c = loads(rk[g], pool); fine = np.all(np.delete(c, o, 1) <= C, 1); s = []
        for i in range(8):
            x = rng.integers(-2, 3)
            for v in (C + x, C - x): s.append(pool[rng.choice(np.flatnonzero(fine & (c[:, o] == v)))])
        sd[r, g] = rng.permutation(np.array(s))
    return complete(rng, rk, sd)
def setup_inputs_edges(rng):
    rk, tie = [], []
    for g in range(8):
        t = ranks(rng, 3500); w = rng.permutation(N)[:4]; t[w[0]] = 0; t[N + w[0]] = w[1]; t[w[1]] = 0; t[N + w[1]] = w[0]; t[w[2]] = rng.integers(3500, 4096); t[N + w[2]] = w[0]; t[w[3]] = 4096; rk.append(t)
        tie.append(seed_of(int(w[2]) * (4096 // N) + int(rng.integers(0, 4096 // N)), int(t[w[2]]), (TR + 1) * int(rng.integers(0, K))))
    rk = np.stack(rk); sd = np.stack([np.stack([sixteen(rng, rk[g], (0, (1 << 24) - 1, tie[g])) for g in range(8)]) for r in range(N)])
    d = complete(rng, rk, sd); z = rng.integers(0, 4, (N, 8, M)); thr = np.where(z == 0, 0, np.where(z == 1, 4096, d["thr"])); z = rng.integers(0, 4, (N, 8, M))
    ali = np.where(z == 0, 0, np.where(z == 1, M - 1, np.where(z == 2, np.arange(M), d["ali"])))
    for r in range(N):
        for g in range(8):
            q = owners(rk[g], sd[r, g])[:, ::4]; a, b = hashes(sd[r, g][:, None], ((TR + 1) * np.arange(K) + 1)[None, ::4]); e = (a * M) >> 12
            thr[q, g, e] = b; ali[q, g, e] = M - 1 - e
    d["thr"] = thr.astype(np.int32); d["ali"] = ali.astype(np.int32); return d
def setup_inputs_hot(rng):
    rk = np.stack([ranks(rng, 2800) for g in range(8)]); sd = seeds(rng, rk)
    for g in range(8):
        pool = rng.integers(0, 1 << 24, 1024); sd[rng.integers(0, N), g] = pool[rng.choice(np.flatnonzero(np.all(loads(rk[g], pool) <= CAP // 16, 1)))]
    d = complete(rng, rk, sd); h = rng.integers(0, M, (N, 8, 1)); h[:, 0] = 0; h[:, 7] = M - 1
    d["thr"] = rng.integers(0, 512, (N, 8, M)).astype(np.int32); d["ali"] = (h + np.zeros((1, 1, M), np.int64)).astype(np.int32); return d
def setup_inputs_avid(rng):
    rk = np.stack([absent(rng) for g in range(8)]); dens = rng.choice(np.array([0, 0.97, 1.0]), (N, 128)); dens[rng.integers(0, N)] = 1
    return complete(rng, rk, seeds(rng, rk), dens)
def setup_inputs_spread(rng):
    d = setup_inputs(rng); d["vec"] = wide(rng, N, 128, M); d["thr"] = (4096 >> rng.integers(0, 14, (N, 8, M))).astype(np.int32); return d
def check_inputs(d):
    bad = []
    try:
        sd, rk = d["sd"].astype(np.int64), d["rk"].astype(np.int64); w = d["seen"].astype(np.float32)
        if not ((sd >= 0) & (sd < 1 << 24)).all(): bad.append("seed")
        if not (rk == rk[:1]).all(): bad.append("rk alike on all ranks")
        if not ((rk[..., :N] >= 0) & (rk[..., :N] <= 4096) & (rk[..., N:] >= 0) & (rk[..., N:] < N)).all(): bad.append("rk")
        if not ((d["thr"] >= 0) & (d["thr"] <= 4096)).all(): bad.append("thr")
        if not ((d["ali"] >= 0) & (d["ali"] < M)).all(): bad.append("ali")
        if not ((w >= 0) & (w < 2 ** N) & (w == np.floor(w))).all(): bad.append("seen")
        if not np.isfinite(d["vec"].astype(np.float32)).all(): bad.append("finite")
        if not bad and any((np.sum(loads(rk[r, g], sd[r, 16 * g:16 * g + 16, 0]), 0) > CAP).any() for r in range(N) for g in range(8)): bad.append("cap")
    except Exception:
        bad.append("unreadable")
    return bad
def reference(sd, rk, thr, ali, seen, vec):
    chosen = np.zeros((N, 128, K), np.float32); y = np.zeros((N, 128, D), vec.dtype); n = (TR + 1) * np.arange(K); row = np.arange(16)[:, None]
    for r in range(N):
        for g in range(8):
            s = sd[r, 16 * g:16 * g + 16].astype(np.int64)
            q = owners(rk[r, g].astype(np.int64), s[:, 0])
            x = np.zeros((16, K), np.int64); done = np.zeros((16, K), bool)
            for i in range(1, TR + 1):
                a, b = hashes(s, n + i); e = (a * M) >> 12
                c = np.where(b < thr[q, g, e], e, ali[q, g, e]).astype(np.int64)
                known = (seen[q, 16 * g + row, c].astype(np.float32).astype(np.int64) >> r) & 1
                x = np.where(done, x, c); done = done | (known == 0)
            chosen[r, 16 * g:16 * g + 16] = q * M + x
            y[r, 16 * g:16 * g + 16] = vec[q.T.reshape(-1), 16 * g + row, x.T.reshape(-1)]
    return {"chosen": chosen, "y": y}

@@ -1,0 +1,446 @@
+from concourse.bass import DstId, RemoteDMATransfer
+from concourse.mybir import AluOpType, ActivationFunctionType
+
+A = AluOpType
+F = ActivationFunctionType
+N = 8
+DIST = [1, 3, 5, 7, 2, 4, 6, 0]
+CAPQ, LC = 192, 12
+CH = [(0, 2), (2, 4), (4, 6), (6, 8)]
+GRP = [(0, 1), (2, 3), (4, 5), (6,)]
+PLAN = [("H", 0, 2), ("H", 2, 8), ("A", 0), ("Y",), ("A", 1), ("F", 0), ("A", 2), ("F", 1), ("P", 0), ("A", 3), ("F", 2), ("P", 1), ("F", 3), ("P", 2), ("P", 3),
+        ("I", 0), ("I", 1), ("I", 2), ("I", 3)]
+MW, RW = 52, 216
+f32, b16, i32, u16 = "float32", "bfloat16", "int32", "uint16"
+SCRATCH = {
+    "sdI": ("sbuf", [128, 1], i32), "rkI": ("sbuf", [128, 16], i32), "rkF": ("sbuf", [128, 16], f32),
+    "thrI": ("sbuf", [128, 128], i32), "aliI": ("sbuf", [128, 128], i32),
+    "seenS": ("sbuf", [128, 2048], b16), "vecS": ("sbuf", [128, 2048], b16), "W1": ("sbuf", [128, 2048], b16),
+    "onef": ("sbuf", [128, 144], f32), "oneb": ("sbuf", [128, 128], b16), "iotaK": ("sbuf", [128, 64], i32),
+    "Rm": ("sbuf", [128, 128], f32), "Id": ("sbuf", [128, 128], b16), "Id192": ("sbuf", [128, 128], b16),
+    "Tri": ("sbuf", [128, 128], b16), "IdF": ("sbuf", [128, 144], f32), "rst": ("sbuf", [128, 512], b16),
+    "Zs": ("sbuf", [128, 144], b16), "Za": ("sbuf", [128, 144], b16), "Zb": ("sbuf", [128, 144], b16), "Zt": ("sbuf", [128, 144], b16), "Zi": ("sbuf", [128, 144], b16),
+    "jc": ("sbuf", [128, 192], b16), "eIo": ("sbuf", [128, 128], i32), "w1c": ("sbuf", [128, 8], f32), "w4c": ("sbuf", [128, 8], f32),
+    "loI": ("sbuf", [128, 1], i32), "hiI": ("sbuf", [128, 1], i32), "loF": ("sbuf", [128, 1], f32), "hiF": ("sbuf", [128, 1], f32), "hpF": ("sbuf", [128, 1], f32),
+    "Lr": ("sbuf", [128, 64], i32), "Lq": ("sbuf", [128, 64], i32), "Vp": ("sbuf", [128, 64], f32), "t1": ("sbuf", [128, 64], i32), "Bq": ("sbuf", [128, 64], i32),
+    "Lp": ("sbuf", [128, 64], i32), "t2": ("sbuf", [128, 64], i32), "w12": ("sbuf", [128, 64], i32), "Zk": ("sbuf", [128, 64], f32),
+    "tA": ("sbuf", [128, 8], f32), "dA": ("sbuf", [128, 8], f32), "dB": ("sbuf", [128, 8], f32), "stp": ("sbuf", [128, 1024], b16),
+    "Pc": ("sbuf", [128, 512], b16), "Dc": ("sbuf", [128, 512], b16), "Of": ("sbuf", [128, 512], b16), "ownb": ("sbuf", [128, 64], b16),
+    "F2u": ("sbuf", [128, 64], u16), "VxS": ("sbuf", [128, 1024], f32), "Vwin": ("sbuf", [128, 1536], f32), "vl": ("sbuf", [128, 8, 12], f32),
+    "F2i": ("sbuf", [128, 64], i32), "ya": ("sbuf", [128, 64], i32), "yb": ("sbuf", [128, 64], i32), "yc": ("sbuf", [128, 64], i32), "yd": ("sbuf", [128, 64], i32),
+    "yo": ("sbuf", [128, 64], u16), "own2k": ("sbuf", [128, 64], f32), "own200": ("sbuf", [128, 64], i32), "ot": ("sbuf", [128, 8], f32),
+    "T0": ("sbuf", [128, 128], f32), "T1": ("sbuf", [128, 128], f32), "T2": ("sbuf", [128, 128], f32), "r1": ("sbuf", [128, 128], f32), "eW": ("sbuf", [128, 128], i32),
+    "p0": ("sbuf", [128, 128], b16), "p1": ("sbuf", [128, 128], b16), "p2": ("sbuf", [128, 128], b16), "p3": ("sbuf", [128, 128], b16), "p4": ("sbuf", [128, 128], b16),
+    "hx": ("sbuf", [128, 8, 48], i32), "hL": ("sbuf", [128, 8, 48], i32), "h4": ("sbuf", [128, 8, 48], i32), "hq": ("sbuf", [128, 8, 48], i32), "ht": ("sbuf", [128, 8, 48], i32),
+    "hB": ("sbuf", [128, 8, 48], i32), "hb": ("sbuf", [128, 8, 48], i32), "hu": ("sbuf", [128, 8, 48], i32), "he": ("sbuf", [128, 8, 48], i32),
+    "msg": ("sbuf", [128, 8, MW], i32), "rq": ("sbuf", [128, 8, MW], i32),
+    "nbh": ("sbuf", [128, 16], f32), "ab": ("sbuf", [128, 1536], b16), "mk": ("sbuf", [128, 1536], b16), "eI": ("sbuf", [128, 8, 48], i32), "le": ("sbuf", [128, 384], u16),
+    "GT": ("sbuf", [128, 6144], b16), "mn": ("sbuf", [128, 8, 48], i32), "cI": ("sbuf", [128, 8, 48], i32), "ls": ("sbuf", [128, 288], u16), "MG": ("sbuf", [128, 4608], b16),
+    "sI": ("sbuf", [128, 288], i32), "sb": ("sbuf", [128, 288], i32), "ky": ("sbuf", [128, 288], i32),
+    "ka": ("sbuf", [128, 96], i32), "kb": ("sbuf", [128, 96], i32), "kc": ("sbuf", [128, 96], i32), "xI": ("sbuf", [128, 96], i32), "lx": ("sbuf", [128, 96], u16),
+    "rs": ("sbuf", [128, 8, RW], b16), "land": ("sbuf", [128, 8 * RW], b16),
+    "xf": ("sbuf", [128, 96], f32), "xu": ("sbuf", [128, 96], u16), "IDx": ("sbuf", [128, 8 * RW], b16), "IDg": ("sbuf", [128, 1024], b16),
+    "yS": ("sbuf", [128, 1024], b16), "chS": ("sbuf", [128, 64], f32),
+}
+for _b in range(8):
+    SCRATCH["b%d" % _b] = ("psum", [128, 512], f32)
+SEMAPHORES = ["sv", "ss", "st", "sg", "lsem"] + ["d%d" % _k for _k in range(32)] + ["rq%d" % _k for _k in range(N)] + ["la%d" % _k for _k in range(N)]
+
+
+def rank_program(g, core, T, topo):
+    me = T.rank_of(core)
+    if me is None:
+        return
+    queue = {"v": g.vector, "s": g.scalar, "t": g.tensor, "g": g, "y": g.sync}
+    count = {}
+    clock = {q: {} for q in queue}
+    seen_by = {}
+    log = {}
+    ndma = [0]
+
+    def V2(name, a=0, b=None, step=1, p=None, key=None):
+        b = SCRATCH[name][1][1] if b is None else b
+        ap = T[name][:, a:b:step] if p is None else T[name][p, a:b:step]
+        return (ap, [(key or name, a, b)])
+
+    def V3(name, s0, s1, a, b):
+        w = SCRATCH[name][1][2]
+        ap = T[name][:, s0, a:b] if s1 == s0 + 1 else T[name][:, s0:s1, a:b]
+        return (ap, [(name, s * w + a, s * w + b) for s in range(s0, s1)])
+
+    def IX(win, off):
+        return (win[0].indirect(off[0]), win[1] + off[1])
+
+    BANKS = ["b%d" % k for k in range(8)]
+
+    def need(q, reads, writes):
+        toks = []
+        for regs, w in ((reads, False), (writes, True)):
+            for (k, lo, hi) in regs:
+                for (l2, h2, w2, tok, e2) in log.get(k, []):
+                    if k in BANKS and e2 != q:
+                        toks.append(tok)
+                    elif l2 < hi and lo < h2 and (w or w2) and not (q == "t" and e2 == "t"):
+                        toks.append(tok)
+        best = {}
+        for (s, n) in toks:
+            if clock[q].get(s, 0) < n:
+                best[s] = max(best.get(s, 0), n)
+        for s in sorted(best, key=lambda s: (s[0] != "d", s)):
+            n = best[s]
+            if clock[q].get(s, 0) < n:
+                queue[q].wait_ge(T.sem[s], n)
+                clock[q][s] = n
+                for s2, n2 in seen_by.get((s, n), {}).items():
+                    clock[q][s2] = max(clock[q].get(s2, 0), n2)
+
+    def done(q, inst, reads, writes, sem, inc):
+        inst.then_inc(T.sem[sem], inc)
+        count[sem] = count.get(sem, 0) + inc
+        tok = (sem, count[sem])
+        c = dict(clock[q])
+        c[sem] = count[sem]
+        seen_by[tok] = c
+        for regs, w in ((reads, False), (writes, True)):
+            for (k, lo, hi) in regs:
+                log.setdefault(k, []).append((lo, hi, w, tok, q))
+
+    def op(q, f, outs, ins):
+        reads = [r for x in ins for r in x[1]]
+        writes = [r for x in outs for r in x[1]]
+        need(q, reads, writes)
+        done(q, f(), reads, writes, "s" + q, 1)
+
+    def isv(x):
+        return isinstance(x, tuple)
+
+    def raw(x):
+        return x[0] if isv(x) else x
+
+    def ts(out, in0, s1, s2, o0, o1=None):
+        ins = [x for x in (in0, s1, s2) if isv(x)]
+        if o1 is None:
+            op("v", lambda: g.vector.tensor_scalar(out[0], in0[0], raw(s1), None, o0), [out], ins)
+        else:
+            op("v", lambda: g.vector.tensor_scalar(out[0], in0[0], raw(s1), raw(s2), o0, o1), [out], ins)
+
+    def tt(out, a, b, o):
+        op("v", lambda: g.vector.tensor_tensor(out[0], a[0], b[0], o), [out], [a, b])
+
+    def cp(out, a):
+        op("v", lambda: g.vector.tensor_copy(out[0], a[0]), [out], [a])
+
+    def fill(out, c):
+        op("v", lambda: g.vector.memset(out[0], c), [out], [])
+
+    def act(out, a, func=F.Copy, **kw):
+        ins = [a] + [x for x in kw.values() if isv(x)]
+        k2 = {k: raw(x) for k, x in kw.items()}
+        op("s", lambda: g.scalar.activation(out[0], a[0], func, **k2), [out], ins)
+
+    def mm(out, lhs, rhs, start, stop):
+        op("t", lambda: g.tensor.matmul(out[0], lhs[0], rhs[0], start, stop), [out], [lhs, rhs])
+
+    def aff(out, a, pat, cmp, base, cm):
+        op("g", lambda: g.affine_select(out[0], a[0], pat, cmp, 0.0, base, cm), [out], [a])
+
+    def iota(out, pat, base, cm, small=False):
+        if small:
+            op("g", lambda: g.iota(out[0], pat, base, cm, allow_small_or_imprecise_dtypes=True), [out], [])
+        else:
+            op("g", lambda: g.iota(out[0], pat, base, cm), [out], [])
+
+    def dma(q, out, a):
+        need(q, a[1], out[1])
+        sem = "d%d" % ndma[0]
+        ndma[0] += 1
+        done(q, queue[q].dma_start(out[0], a[0]), a[1], out[1], sem, 16)
+
+    def hbm(ap):
+        return (ap, [])
+
+    def send(pairs, sem):
+        need("g", [r for x in pairs for r in x[2][1]], [])
+        tr = []
+        for j, (s, q, a, o) in enumerate(pairs):
+            eng = topo.engines(core, T.cores[q])
+            n = len(eng) // len(pairs)
+            rid, pid, se = topo.addr(T.cores[q])
+            count["lsem"] = count.get("lsem", 0) + n
+            if len(pairs) == 1:
+                g.remote_dma(o, a[0], T.sem["%s%d" % (sem, s)], T.sem.lsem, pid, rid, topo.mask(core, T.cores[q]))
+                return
+            tr.append(RemoteDMATransfer(dst_ids=[DstId(rid=rid, pnc=pid)], dma_engine_mask=sum(1 << e for e in eng[n * j:n * j + n]),
+                                        remote_sem=T.sem["%s%d" % (sem, s)], src=a[0], dst=o))
+        g.remote_dma_fused(tr, local_sem=T.sem.lsem)
+
+    owner = [(me + d) % N for d in DIST]
+    asker = [(me - d) % N for d in DIST]
+    S0 = DIST.index(0)
+
+    def arrives(sem, s, src, view):
+        n = len(topo.engines(T.cores[src], core)) // [len(gr) for gr in GRP if s in gr][0]
+        name = "%s%d" % (sem, s)
+        count[name] = n
+        seen_by[(name, n)] = {name: n}
+        for (k, lo, hi) in view[1]:
+            log.setdefault(k, []).append((lo, hi, True, (name, n), "remote"))
+
+    for s in range(N):
+        if s != S0:
+            arrives("rq", s, asker[s], V3("rq", s, s + 1, 0, 50))
+            arrives("la", s, owner[s], V2("land", RW * owner[s], RW * owner[s] + RW))
+
+    dma("y", V2("sdI"), hbm(T.sd[:]))
+    dma("s", V2("rkI", p=slice(0, 8)), hbm(T.rk[:]))
+    dma("y", V2("thrI"), hbm(T.thr[:]))
+    dma("s", V2("aliI"), hbm(T.ali[:]))
+    dma("y", V2("seenS"), hbm(T.seen[:]))
+    dma("y", V2("vecS"), hbm(T.vec[:]))
+
+    fill(V2("onef"), 1.0)
+    fill(V2("oneb"), 1.0)
+    fill(V2("Zs"), 0.0)
+    fill(V2("rst"), 1.0)
+    fill(V2("Zs", 15, 144, 16), 1.0)
+    fill(V2("rst", 0, 512, 64), 0.0)
+    fill(V2("Vwin"), 0.0)
+    iota(V2("iotaK"), [[7985, 64]], 0, 0)
+    iota(V2("w1c"), [[1, 8]], 0, 0, True)
+    iota(V2("w4c"), [[4096, 8]], 0, 0, True)
+    P8 = slice(0, 8)
+    aff(V2("Rm", p=P8), V2("onef", 0, 128, p=P8), [[1, 128]], A.is_ge, 0, -16)
+    aff(V2("Rm", p=P8), V2("Rm", p=P8), [[-1, 128]], A.is_ge, 15, 16)
+    aff(V2("IdF"), V2("onef"), [[-1, 144]], A.is_equal, 0, 1)
+    aff(V2("Id"), V2("oneb"), [[-1, 128]], A.is_equal, 0, 1)
+    aff(V2("Tri"), V2("oneb"), [[16, 8], [1, 16]], A.is_gt, 0, -1)
+    aff(V2("Tri"), V2("Tri"), [[-16, 8], [0, 16]], A.is_ge, 0, 1)
+    iota(V2("eIo"), [[1, 128]], 0, 128)
+    aff(V2("Za"), V2("Zs"), [[-16, 9], [0, 16]], A.is_ge, 0, 1)
+    aff(V2("Zs"), V2("Za"), [[16, 9], [0, 16]], A.is_ge, 15, -1)
+    aff(V2("Zt"), V2("Za"), [[16, 9], [0, 16]], A.is_ge, 2, -1)
+    iota(V2("jc"), [[2, LC], [2 * LC, 16]], 0, 0, True)
+    aff(V2("Zb"), V2("Zs"), [[-16, 9], [0, 16]], A.is_ge, -3, 1)
+    aff(V2("Zi"), V2("Zb"), [[16, 9], [0, 16]], A.is_ge, 4, -1)
+
+    def Z(name, i):
+        return V2(name, 15 - i, 143 - i)
+
+    cp(V2("rkF", p=P8), V2("rkI", p=P8))
+    ts(V2("loI"), V2("sdI"), 4095, None, A.bitwise_and)
+    ts(V2("hiI"), V2("sdI"), 12, None, A.arith_shift_right)
+    mm(V2("b4", 0, 16), V2("Rm", p=P8), V2("rkF", p=P8), True, True)
+    cp(V2("loF"), V2("loI"))
+    cp(V2("hiF"), V2("hiI"))
+    ts(V2("Lr"), V2("iotaK"), V2("loF"), None, A.add)
+    ts(V2("hpF"), V2("hiI"), 64.0, -262144.0, A.mult, A.add)
+    ts(V2("Lq"), V2("Lr"), 4095, None, A.bitwise_and)
+    tt(V2("b6", 0, 64), V2("Lq"), V2("Lq"), A.mult)
+    ts(V2("Vp"), V2("Lq"), 4096.0, V2("hiF"), A.mult, A.add)
+    ts(V2("t1"), V2("b6", 0, 64), V2("hpF"), None, A.add)
+    ts(V2("Lp"), V2("Lq"), 64.0, -262144.0, A.mult, A.add)
+    ts(V2("Bq"), V2("t1"), 6, 4095, A.arith_shift_right, A.bitwise_and)
+    tt(V2("tA"), V2("w4c"), V2("b4", 0, 8), A.add)
+    tt(V2("b6", 64, 128), V2("Bq"), V2("Bq"), A.mult)
+    tt(V2("dA"), V2("b4", 8, 16), V2("w1c"), A.subtract)
+    tt(V2("t2"), V2("Lp"), V2("b6", 64, 128), A.add)
+    ts(V2("dB"), V2("dA"), -1.0, 1.0, A.mult, A.add)
+    ts(V2("w12"), V2("t2"), 3, 28672, A.arith_shift_right, A.bitwise_and)
+    tt(V2("Zk"), V2("w12"), V2("Bq"), A.add)
+
+    xb = ["b0", "b1", "b7"]
+
+    def spread(us):
+        for u in us:
+            mm(V2(xb[u // 2 % 3], 64 * (u % 2), 64 * (u % 2) + 64), V2("IdF", u, u + 128), V2("Vp"), True, True)
+            if u % 2:
+                for w in (u - 1, u):
+                    act(V2("VxS", w, 1024, 16, key="VxS%d" % w), V2(xb[u // 2 % 3], 64 * (w % 2), 64 * (w % 2) + 64))
+
+    act(V2("Id192"), V2("Id"), scale=192.0)
+    spread(range(0, 4))
+    own = V2("b3", 0, 64)
+    k = 0
+    for w in range(8):
+        ts(V2("stp", 64 * k, 64 * k + 64), V2("Zk"), V2("tA", w, w + 1), V2("dA", w, w + 1), A.is_ge, A.mult)
+        k += 1
+        if w < 7:
+            ts(V2("stp", 64 * k, 64 * k + 64), V2("Zk"), 4096.0 * (w + 1), V2("dB", w, w + 1), A.is_ge, A.mult)
+            k += 1
+    for j in range(15):
+        mm(own, V2("Id"), V2("stp", 64 * j, 64 * j + 64), j == 0, j == 14)
+    spread(range(4, 8))
+    for s in range(N):
+        ts(V2("b2", 64 * s, 64 * s + 64), own, float(owner[s]), None, A.is_equal)
+    op("v", lambda: g.vector.tensor_tensor_scan(T.Pc[:], T.rst[:], T.b2[:], 0.0, A.mult, A.add), [V2("Pc")], [V2("rst"), V2("b2")])
+    cp(V2("ownb"), own)
+    tt(V2("Dc"), V2("Pc"), V2("b2"), A.mult)
+    cnt = V2("Pc", 63, 512, 64)
+    mm(V2("b4", 16, 24), V2("Tri"), cnt, True, True)
+    f2 = V2("b5", 0, 64)
+    mm(f2, V2("Id192"), V2("ownb"), True, False)
+    spread(range(8, 10))
+    for s in range(N):
+        mm(f2, V2("Id"), V2("Dc", 64 * s, 64 * s + 64), False, False)
+    for s in range(N):
+        ts(V2("Of", 64 * s, 64 * s + 64), V2("ownb"), float(owner[s]), V2("b4", 16 + s, 17 + s), A.is_equal, A.mult)
+        mm(f2, V2("Id"), V2("Of", 64 * s, 64 * s + 64), False, s == N - 1)
+    spread(range(10, 16))
+    for z in range(4):
+        act(V2("W1", 512 * z, 512 * z + 512), V2("rst"), scale=0.0)
+    ts(V2("F2u"), f2, -1.0, None, A.add)
+
+    ts(V2("T0"), V2("thrI"), 4096.0, None, A.mult)
+    tt(V2("T1"), V2("T0"), V2("aliI"), A.add)
+    ts(V2("T2"), V2("T1"), 16777216.0, None, A.min)
+    cp(V2("p0"), V2("T2"))
+    tt(V2("r1"), V2("T2"), V2("p0"), A.subtract)
+    cp(V2("p1"), V2("r1"))
+    tt(V2("p2"), V2("r1"), V2("p1"), A.subtract)
+
+    vxs = (T.VxS[:], [("VxS%d" % u, u, 1024) for u in range(16)])
+    cp(IX(V2("Vwin"), V2("F2u")), vxs)
+    for s in range(N):
+        q = owner[s]
+        dma("ys"[s % 2], V3("vl", s, s + 1, 0, LC), (T.Vwin[0:128:16, CAPQ * q:CAPQ * q + CAPQ], [("Vwin", CAPQ * q, CAPQ * q + CAPQ)]))
+    for z in range(4):
+        act(V2("IDx", 432 * z, 432 * z + 432), V2("rst", 0, 432), scale=0.0)
+
+    ts((T.msg[:, :, 49], [("msg", MW * s + 49, MW * s + 50) for s in range(N)]), cnt, 1.0, None, A.mult)
+    ts(V2("ot"), V2("b4", 16, 24), -2.0, 1.0, A.mult, A.add)
+    tt((T.msg[:, :, 48], [("msg", MW * s + 48, MW * s + 49) for s in range(N)]), V2("ot"), cnt, A.subtract)
+    ts(V2("eW"), V2("eIo"), 2047, None, A.bitwise_and)
+    cp(V2("p3"), V2("eW"))
+    tt(V2("p4"), V2("eW"), V2("p3"), A.subtract)
+    for j in range(5):
+        need("y", [], [("W1", 0, 2048)])
+        dma("y", (T.W1[j:128:16, :], [("W1p%d" % j, 0, 2048)]), V2("p%d" % j))
+    tab = (T.W1[:], [("W1", 0, 2048)] + [("W1p%d" % j, 0, 2048) for j in range(5)])
+
+    def ylist():
+        ts(V2("F2i"), f2, -1.0, None, A.add)
+        ts(V2("own200"), V2("ownb"), 200.0, None, A.mult)
+        ts(V2("own2k"), V2("ownb"), 2048.0, None, A.mult)
+        ts(V2("ya"), V2("F2i"), 10923.0, None, A.mult)
+        ts(V2("yc"), V2("F2i"), 16.0, None, A.mult)
+        ts(V2("yb"), V2("ya"), 17, None, A.arith_shift_right)
+        tt(V2("yc"), V2("yc"), V2("own200"), A.add)
+        ts(V2("yb"), V2("yb"), -191.0, None, A.mult)
+        tt(V2("yd"), V2("yb"), V2("yc"), A.add)
+        cp(V2("yo"), V2("yd"))
+
+    def hashes(a, b):
+        def W(nm):
+            return V3(nm, a, b, 0, 48)
+        for i in range(4):
+            kk = ((1597 * (i + 1)) & 4095) - 4096
+            ts(V3("hx", a, b, LC * i, LC * i + LC), V3("vl", a, b, 0, LC), 4096.0 * kk, None, A.add)
+        ts(W("hL"), W("hx"), 12, 4095, A.arith_shift_right, A.bitwise_and)
+        ts(W("h4"), W("hx"), 4095, None, A.bitwise_and)
+        tt(W("hq"), W("hL"), W("hL"), A.mult)
+        p = V2("b6", 0, 48 * (b - a))
+        ts(p, W("h4"), 64.0, -262144.0, A.mult, A.add)
+        tt(W("ht"), W("hq"), p, A.add)
+        ts(p, W("hL"), 64.0, -262144.0, A.mult, A.add)
+        ts(W("hB"), W("ht"), 6, 4095, A.arith_shift_right, A.bitwise_and)
+        tt(W("hb"), W("hB"), W("hB"), A.mult)
+        tt(W("hu"), W("hb"), p, A.add)
+        ts(p, W("hB"), 4096.0, 2048.0, A.mult, A.add)
+        ts(W("he"), W("hu"), 7, 2047, A.arith_shift_right, A.bitwise_and)
+        tt(W("msg"), W("he"), p, A.add)
+        for gr in GRP:
+            if a <= gr[0] < b:
+                send([(s, owner[s], V3("msg", s, s + 1, 0, 50), T.rq[:, s, 0:50]) for s in gr], "rq")
+
+    def arrive(c):
+        a, b = CH[c]
+        if a <= S0 < b:
+            cp(V3("rq", S0, S0 + 1, 0, 50), V3("msg", S0, S0 + 1, 0, 50))
+        ts(V3("eI", a, b, 0, 48), V3("rq", a, b, 0, 48), 2047, None, A.bitwise_and)
+        cp(V2("le", 48 * a, 48 * b), V3("eI", a, b, 0, 48))
+        cp(V2("nbh", 2 * a, 2 * b), V3("rq", a, b, 48, 50))
+        act(V2("GT", 768 * a, 768 * b), IX(tab, V2("le", 48 * a, 48 * b)))
+        for s in range(a, b):
+            act(V2("ab", CAPQ * s, CAPQ * s + CAPQ), V2("jc"), F.Abs, bias=V2("nbh", 2 * s, 2 * s + 1))
+        for i in range(16):
+            mm(V2("b%d" % (c % 2), 0, 48 * (b - a)), Z("Zt", i), V2("GT", 768 * a + i, 768 * b, 16), i == 0, i == 15)
+
+    def filt(c):
+        a, b = CH[c]
+        n = LC * (b - a)
+        tt(V3("mn", a, b, 0, 48), V3("rq", a, b, 0, 48), V2("b%d" % (c % 2), 0, 4 * n), A.min)
+        ts(V3("cI", a, b, 0, 48), V3("mn", a, b, 0, 48), 2047, None, A.bitwise_and)
+        for s in range(a, b):
+            ts(V2("mk", CAPQ * s, CAPQ * s + CAPQ), V2("ab", CAPQ * s, CAPQ * s + CAPQ), V2("nbh", 2 * s + 1, 2 * s + 2), float(2 ** (14 - asker[s])), A.is_lt, A.mult)
+
+        def L(i):
+            return V2("ls", 36 * a + n * i, 36 * a + n * i + n)
+        for i in range(3):
+            cp(L(i), V3("cI", a, b, LC * i, LC * i + LC))
+        for i in range(3):
+            o = 576 * a + 16 * n * i
+            tt(V2("MG", o, o + 16 * n), IX(V2("seenS"), L(i)), V2("mk", CAPQ * a, CAPQ * b), A.mult)
+        for i in range(16):
+            mm(V2("b%d" % (2 + c % 2), 0, 3 * n), Z("Zs", i), V2("MG", 576 * a + i, 576 * b, 16), i == 0, i == 15)
+        for i in range(4):
+            ts(V2("b7", 48 * a + n * i, 48 * a + n * i + n), V3("cI", a, b, LC * i, LC * i + LC), 2048.0 * i, None, A.add)
+
+    def pick(c):
+        a, b = CH[c]
+        n = LC * (b - a)
+        h, o = (36 * a, 36 * b), 48 * a
+        cp(V2("sI", *h), V2("b%d" % (2 + c % 2), 0, 3 * n))
+        ts(V2("sb", *h), V2("sI", *h), 16384, None, A.bitwise_and)
+        tt(V2("ky", *h), V2("sb", *h), V2("b7", o, o + 3 * n), A.add)
+        x, h = (LC * a, LC * b), 36 * a
+        tt(V2("ka", *x), V2("ky", h, h + n), V2("ky", h + n, h + 2 * n), A.min)
+        tt(V2("kb", *x), V2("ky", h + 2 * n, h + 3 * n), V2("b7", o + 3 * n, o + 4 * n), A.min)
+        tt(V2("kc", *x), V2("ka", *x), V2("kb", *x), A.min)
+        ts(V2("xI", *x), V2("kc", *x), 2047, None, A.bitwise_and)
+        cp(V2("lx", *x), V2("xI", *x))
+        for s in range(a, b):
+            R = V2("land", RW * me, RW * me + 192) if s == S0 else V3("rs", s, s + 1, 0, 192)
+            act(R, IX(V2("vecS"), V2("lx", LC * s, LC * s + LC)))
+        for (u, w) in ([(a, S0), (S0, S0 + 1), (S0 + 1, b)] if a <= S0 < b else [(a, b)]):
+            if u < w:
+                hi = V2("land", RW * me + 192, RW * me + 204) if u == S0 else V3("rs", u, w, 192, 204)
+                lo = V2("land", RW * me + 204, RW * me + 216) if u == S0 else V3("rs", u, w, 204, 216)
+                xs = V2("xI", LC * u, LC * w)
+                cp(hi, xs)
+                tt(lo, xs, hi, A.subtract)
+        for gr in GRP:
+            if a <= gr[0] < b:
+                send([(s, asker[s], V3("rs", s, s + 1, 0, RW), T.land[:, RW * me:RW * me + RW]) for s in gr], "la")
+
+    def items(c):
+        a, b = CH[c]
+        for s in range(a, b):
+            o = RW * owner[s]
+            tt(V2("xf", LC * s, LC * s + LC), V2("land", o + 192, o + 204), V2("land", o + 204, o + 216), A.add)
+        cp(V2("xu", LC * a, LC * b), V2("xf", LC * a, LC * b))
+        for s in range(a, b):
+            o = RW * owner[s]
+            act(V2("IDx", o, o + 192), IX(tab, V2("xu", LC * s, LC * s + LC)))
+
+    for (f, *x) in PLAN:
+        {"H": hashes, "A": arrive, "F": filt, "P": pick, "I": items, "Y": ylist}[f](*x)
+
+    def ygat(h):
+        return V2("yS", 512 * h, 512 * h + 512), IX(V2("land"), V2("yo", 32 * h, 32 * h + 32))
+
+    def igat(h):
+        return V2("IDg", 512 * h, 512 * h + 512), IX(V2("IDx"), V2("yo", 32 * h, 32 * h + 32))
+    cp(*ygat(0))
+    dma("y", hbm(T.y[:, 0:512]), V2("yS", 0, 512))
+    act(*igat(0))
+    cp(*igat(1))
+    act(*ygat(1))
+    dma("y", hbm(T.y[:, 512:1024]), V2("yS", 512, 1024))
+    for i in range(16):
+        mm(V2("b4", 64, 128), Z("Zi", i), V2("IDg", i, 1024, 16), i == 0, i == 15)
+    tt(V2("chS"), V2("own2k"), V2("b4", 64, 128), A.add)
+    dma("s", hbm(T.chosen[:]), V2("chS"))
+
+    for s, n in count.items():
+        if clock["g"].get(s, 0) < n:
+            g.wait_ge(T.sem[s], n)

@@ -4,47 +4,38 @@ from concourse.mybir import AluOpType, ActivationFunctionType
 A = AluOpType
 F = ActivationFunctionType
 N = 8
-DIST = [1, 3, 5, 7, 2, 4, 6, 0]
+DIST = [1, 3, 0, 5, 7, 2, 4, 6]
 CAPQ, LC = 192, 12
-CH = [(0, 2), (2, 4), (4, 6), (6, 8)]
-GRP = [(0, 1), (2, 3), (4, 5), (6,)]
-PLAN = [("H", 0, 2), ("H", 2, 8), ("A", 0), ("Y",), ("A", 1), ("F", 0), ("A", 2), ("F", 1), ("P", 0), ("A", 3), ("F", 2), ("P", 1), ("F", 3), ("P", 2), ("P", 3),
-        ("I", 0), ("I", 1), ("I", 2), ("I", 3)]
-MW, RW = 52, 216
-f32, b16, i32, u16 = "float32", "bfloat16", "int32", "uint16"
-SCRATCH = {
-    "sdI": ("sbuf", [128, 1], i32), "rkI": ("sbuf", [128, 16], i32), "rkF": ("sbuf", [128, 16], f32),
-    "thrI": ("sbuf", [128, 128], i32), "aliI": ("sbuf", [128, 128], i32),
-    "seenS": ("sbuf", [128, 2048], b16), "vecS": ("sbuf", [128, 2048], b16), "W1": ("sbuf", [128, 2048], b16),
-    "onef": ("sbuf", [128, 144], f32), "oneb": ("sbuf", [128, 128], b16), "iotaK": ("sbuf", [128, 64], i32),
-    "Rm": ("sbuf", [128, 128], f32), "Id": ("sbuf", [128, 128], b16), "Id192": ("sbuf", [128, 128], b16),
-    "Tri": ("sbuf", [128, 128], b16), "IdF": ("sbuf", [128, 144], f32), "rst": ("sbuf", [128, 512], b16),
-    "Zs": ("sbuf", [128, 144], b16), "Za": ("sbuf", [128, 144], b16), "Zb": ("sbuf", [128, 144], b16), "Zt": ("sbuf", [128, 144], b16), "Zi": ("sbuf", [128, 144], b16),
-    "jc": ("sbuf", [128, 192], b16), "eIo": ("sbuf", [128, 128], i32), "w1c": ("sbuf", [128, 8], f32), "w4c": ("sbuf", [128, 8], f32),
-    "loI": ("sbuf", [128, 1], i32), "hiI": ("sbuf", [128, 1], i32), "loF": ("sbuf", [128, 1], f32), "hiF": ("sbuf", [128, 1], f32), "hpF": ("sbuf", [128, 1], f32),
-    "Lr": ("sbuf", [128, 64], i32), "Lq": ("sbuf", [128, 64], i32), "Vp": ("sbuf", [128, 64], f32), "t1": ("sbuf", [128, 64], i32), "Bq": ("sbuf", [128, 64], i32),
-    "Lp": ("sbuf", [128, 64], i32), "t2": ("sbuf", [128, 64], i32), "w12": ("sbuf", [128, 64], i32), "Zk": ("sbuf", [128, 64], f32),
-    "tA": ("sbuf", [128, 8], f32), "dA": ("sbuf", [128, 8], f32), "dB": ("sbuf", [128, 8], f32), "stp": ("sbuf", [128, 1024], b16),
-    "Pc": ("sbuf", [128, 512], b16), "Dc": ("sbuf", [128, 512], b16), "Of": ("sbuf", [128, 512], b16), "ownb": ("sbuf", [128, 64], b16),
-    "F2u": ("sbuf", [128, 64], u16), "VxS": ("sbuf", [128, 1024], f32), "Vwin": ("sbuf", [128, 1536], f32), "vl": ("sbuf", [128, 8, 12], f32),
-    "F2i": ("sbuf", [128, 64], i32), "ya": ("sbuf", [128, 64], i32), "yb": ("sbuf", [128, 64], i32), "yc": ("sbuf", [128, 64], i32), "yd": ("sbuf", [128, 64], i32),
-    "yo": ("sbuf", [128, 64], u16), "own2k": ("sbuf", [128, 64], f32), "own200": ("sbuf", [128, 64], i32), "ot": ("sbuf", [128, 8], f32),
-    "T0": ("sbuf", [128, 128], f32), "T1": ("sbuf", [128, 128], f32), "T2": ("sbuf", [128, 128], f32), "r1": ("sbuf", [128, 128], f32), "eW": ("sbuf", [128, 128], i32),
-    "p0": ("sbuf", [128, 128], b16), "p1": ("sbuf", [128, 128], b16), "p2": ("sbuf", [128, 128], b16), "p3": ("sbuf", [128, 128], b16), "p4": ("sbuf", [128, 128], b16),
-    "hx": ("sbuf", [128, 8, 48], i32), "hL": ("sbuf", [128, 8, 48], i32), "h4": ("sbuf", [128, 8, 48], i32), "hq": ("sbuf", [128, 8, 48], i32), "ht": ("sbuf", [128, 8, 48], i32),
-    "hB": ("sbuf", [128, 8, 48], i32), "hb": ("sbuf", [128, 8, 48], i32), "hu": ("sbuf", [128, 8, 48], i32), "he": ("sbuf", [128, 8, 48], i32),
-    "msg": ("sbuf", [128, 8, MW], i32), "rq": ("sbuf", [128, 8, MW], i32),
-    "nbh": ("sbuf", [128, 16], f32), "ab": ("sbuf", [128, 1536], b16), "mk": ("sbuf", [128, 1536], b16), "eI": ("sbuf", [128, 8, 48], i32), "le": ("sbuf", [128, 384], u16),
-    "GT": ("sbuf", [128, 6144], b16), "mn": ("sbuf", [128, 8, 48], i32), "cI": ("sbuf", [128, 8, 48], i32), "ls": ("sbuf", [128, 288], u16), "MG": ("sbuf", [128, 4608], b16),
-    "sI": ("sbuf", [128, 288], i32), "sb": ("sbuf", [128, 288], i32), "ky": ("sbuf", [128, 288], i32),
-    "ka": ("sbuf", [128, 96], i32), "kb": ("sbuf", [128, 96], i32), "kc": ("sbuf", [128, 96], i32), "xI": ("sbuf", [128, 96], i32), "lx": ("sbuf", [128, 96], u16),
-    "rs": ("sbuf", [128, 8, RW], b16), "land": ("sbuf", [128, 8 * RW], b16),
-    "xf": ("sbuf", [128, 96], f32), "xu": ("sbuf", [128, 96], u16), "IDx": ("sbuf", [128, 8 * RW], b16), "IDg": ("sbuf", [128, 1024], b16),
-    "yS": ("sbuf", [128, 1024], b16), "chS": ("sbuf", [128, 64], f32),
+HS = [(0, 2), (2, 5), (5, 8)]
+CH = [(2, 3), (0, 2), (3, 5), (5, 7), (7, 8)]
+GRP = [(0, 1), (3, 4), (5, 6), (7,)]
+PLAN = [[("T",), ("Y",)], ("H", 0), ("H", 1), ("G", 0), ("A", 0), ("G", 1), [("H", 2), ("M", 0, 8)], ("A", 1), ("G", 2), ("F", 0), ("G", 3), ("A", 2), [("F", 1), ("P", 0)],
+        ("A", 3), [("F", 2), ("P", 1)], ("G", 4), ("A", 4), ("I", 0), [("F", 3), ("P", 2)], [("F", 4), ("P", 3)], ("P", 4), ("I", 1), ("I", 2), ("I", 3), ("I", 4)]
+TB = ["b0", "b1", "b7"]
+f32, b16, i32, u16, f16 = "float32", "bfloat16", "int32", "uint16", "float16"
+SHAPES = {
+    i32: {"sdI": 1, "rkI": 16, "thrI": 128, "aliI": 128, "iotaK": 64,
+          "loI": 1, "hiI": 1, "Lr": 64, "Lq": 64, "t1": 64, "Bq": 64, "Lp": 64, "t2": 64, "w12": 64,
+          "F2i": 64, "ya": 64, "yb": 64, "yc": 64, "yd": 64, "own176": 64,
+          "hx": (8, 48), "hL": (8, 48), "h4": (8, 48), "hq": (8, 48), "ht": (8, 48), "hB": (8, 48), "hb": (8, 48), "hu": (8, 48), "he": (8, 48),
+          "mn": (8, 48), "cI": (8, 48), "sI": 288, "sb": (8, 36), "ky": (8, 48), "m2": (8, 24), "kc": 96, "xI": 96},
+    f32: {"rkF": 16, "onef": 128, "Rm": 128, "w1c": 8, "w4c": 8, "loF": 1, "hiF": 1, "hpF": 1, "Zk": 64, "tA": 8, "dA": 8, "dB": 8,
+          "VxS": 1024, "Vwin": 1536, "vl": (8, 12), "own2k": 64, "ot": 8, "T0": 128, "T1": 128, "T2": 128, "r1": 128,
+          "rnS": (8, 2), "rn": (8, 2), "msg": (8, 48), "rq": (8, 48), "chS": 64},
+    b16: {"seenS": 2048, "vecS": 2048, "W1": 2048, "oneb": 144, "Id": 144, "Id192": 128, "Tri": 128, "rst": 512, "Ci": 108,
+          "Zs": 144, "Za": 144, "Zb": 144, "Zt": 144, "Zi": 144, "jc": 192, "stp": 1024, "Pc": 512, "Dc": 512, "Of": 512, "ownb": 64,
+          "p0": 128, "p1": 128, "p2": 128, "p4": 128, "rs": 1536, "land": 1536, "ab": 1536, "mk": 1536, "GT": 6144, "MG": 4608,
+          "IDx": 1536, "IDg": 1024, "yS": 1024},
+    u16: {"F2u": 64, "yo": 64, "le": 384, "rl": 384, "lx": 96, "lr": 96, "ls": 288},
+    f16: {"I1": 144, "I4": 144, "Lh": 64, "Hh": 64},
 }
+SCRATCH = {}
+for _dt, _d in SHAPES.items():
+    for _k, _n in _d.items():
+        SCRATCH[_k] = ("sbuf", [128] + (list(_n) if isinstance(_n, tuple) else [_n]), _dt)
 for _b in range(8):
     SCRATCH["b%d" % _b] = ("psum", [128, 512], f32)
-SEMAPHORES = ["sv", "ss", "st", "sg", "lsem"] + ["d%d" % _k for _k in range(32)] + ["rq%d" % _k for _k in range(N)] + ["la%d" % _k for _k in range(N)]
+SEMAPHORES = ["sv", "ss", "st", "sg", "lsem"] + ["d%d" % _k for _k in range(32)] + ["%s%d" % (_m, _k) for _m in ("rn", "rl", "rq", "lr", "la") for _k in range(N)]
 
 
 def rank_program(g, core, T, topo):
@@ -105,11 +96,22 @@ def rank_program(g, core, T, topo):
             for (k, lo, hi) in regs:
                 log.setdefault(k, []).append((lo, hi, w, tok, q))
 
-    def op(q, f, outs, ins):
+    stream = [None]
+
+    def later(q, f):
+        if stream[0] is None:
+            f()
+        else:
+            stream[0].append((q, f))
+
+    def now(q, f, outs, ins):
         reads = [r for x in ins for r in x[1]]
         writes = [r for x in outs for r in x[1]]
         need(q, reads, writes)
         done(q, f(), reads, writes, "s" + q, 1)
+
+    def op(q, f, outs, ins):
+        later(q, lambda: now(q, f, outs, ins))
 
     def isv(x):
         return isinstance(x, tuple)
@@ -150,16 +152,19 @@ def rank_program(g, core, T, topo):
         else:
             op("g", lambda: g.iota(out[0], pat, base, cm), [out], [])
 
-    def dma(q, out, a):
-        need(q, a[1], out[1])
+    def dma_now(q, out, a, after):
+        need(q, a[1], out[1] + after)
         sem = "d%d" % ndma[0]
         ndma[0] += 1
         done(q, queue[q].dma_start(out[0], a[0]), a[1], out[1], sem, 16)
 
+    def dma(q, out, a, after=()):
+        later(q, lambda: dma_now(q, out, a, list(after)))
+
     def hbm(ap):
         return (ap, [])
 
-    def send(pairs, sem):
+    def send_now(pairs, sem):
         need("g", [r for x in pairs for r in x[2][1]], [])
         tr = []
         for j, (s, q, a, o) in enumerate(pairs):
@@ -174,22 +179,29 @@ def rank_program(g, core, T, topo):
                                         remote_sem=T.sem["%s%d" % (sem, s)], src=a[0], dst=o))
         g.remote_dma_fused(tr, local_sem=T.sem.lsem)
 
+    def send(pairs, sem):
+        later("g", lambda: send_now(pairs, sem))
+
     owner = [(me + d) % N for d in DIST]
     asker = [(me - d) % N for d in DIST]
     S0 = DIST.index(0)
+    FAR = [s for s in range(N) if s != S0]
 
-    def arrives(sem, s, src, view):
-        n = len(topo.engines(T.cores[src], core)) // [len(gr) for gr in GRP if s in gr][0]
+    def arrives(sem, s, src, view, together):
+        n = len(topo.engines(T.cores[src], core)) // together
         name = "%s%d" % (sem, s)
         count[name] = n
         seen_by[(name, n)] = {name: n}
         for (k, lo, hi) in view[1]:
             log.setdefault(k, []).append((lo, hi, True, (name, n), "remote"))
 
-    for s in range(N):
-        if s != S0:
-            arrives("rq", s, asker[s], V3("rq", s, s + 1, 0, 50))
-            arrives("la", s, owner[s], V2("land", RW * owner[s], RW * owner[s] + RW))
+    for s in FAR:
+        k = [len(gr) for gr in GRP if s in gr][0]
+        arrives("rn", s, asker[s], V3("rn", s, s + 1, 0, 2), N - 1)
+        arrives("rl", s, asker[s], V2("rl", 48 * s, 48 * s + 48), k)
+        arrives("rq", s, asker[s], V3("rq", s, s + 1, 0, 48), k)
+        arrives("lr", s, owner[s], V2("lr", LC * s, LC * s + LC), k)
+        arrives("la", s, owner[s], V2("land", CAPQ * owner[s], CAPQ * owner[s] + CAPQ), k)
 
     dma("y", V2("sdI"), hbm(T.sd[:]))
     dma("s", V2("rkI", p=slice(0, 8)), hbm(T.rk[:]))
@@ -198,34 +210,33 @@ def rank_program(g, core, T, topo):
     dma("y", V2("seenS"), hbm(T.seen[:]))
     dma("y", V2("vecS"), hbm(T.vec[:]))
 
-    fill(V2("onef"), 1.0)
     fill(V2("oneb"), 1.0)
-    fill(V2("Zs"), 0.0)
+    fill(V2("onef"), 1.0)
     fill(V2("rst"), 1.0)
-    fill(V2("Zs", 15, 144, 16), 1.0)
     fill(V2("rst", 0, 512, 64), 0.0)
-    fill(V2("Vwin"), 0.0)
+    fill(V2("Zs"), 0.0)
+    fill(V2("Zs", 15, 144, 16), 1.0)
     iota(V2("iotaK"), [[7985, 64]], 0, 0)
     iota(V2("w1c"), [[1, 8]], 0, 0, True)
     iota(V2("w4c"), [[4096, 8]], 0, 0, True)
     P8 = slice(0, 8)
+    aff(V2("Id"), V2("oneb"), [[-1, 144]], A.is_equal, 0, 1)
     aff(V2("Rm", p=P8), V2("onef", 0, 128, p=P8), [[1, 128]], A.is_ge, 0, -16)
     aff(V2("Rm", p=P8), V2("Rm", p=P8), [[-1, 128]], A.is_ge, 15, 16)
-    aff(V2("IdF"), V2("onef"), [[-1, 144]], A.is_equal, 0, 1)
-    aff(V2("Id"), V2("oneb"), [[-1, 128]], A.is_equal, 0, 1)
-    aff(V2("Tri"), V2("oneb"), [[16, 8], [1, 16]], A.is_gt, 0, -1)
+    aff(V2("Tri"), V2("oneb", 0, 128), [[16, 8], [1, 16]], A.is_gt, 0, -1)
     aff(V2("Tri"), V2("Tri"), [[-16, 8], [0, 16]], A.is_ge, 0, 1)
-    iota(V2("eIo"), [[1, 128]], 0, 128)
-    aff(V2("Za"), V2("Zs"), [[-16, 9], [0, 16]], A.is_ge, 0, 1)
-    aff(V2("Zs"), V2("Za"), [[16, 9], [0, 16]], A.is_ge, 15, -1)
-    aff(V2("Zt"), V2("Za"), [[16, 9], [0, 16]], A.is_ge, 2, -1)
+    iota(V2("W1"), [[128, 16], [0, 128]], 0, 0, True)
+    iota(V2("p4"), [[1, 128]], 0, 0, True)
     iota(V2("jc"), [[2, LC], [2 * LC, 16]], 0, 0, True)
-    aff(V2("Zb"), V2("Zs"), [[-16, 9], [0, 16]], A.is_ge, -3, 1)
-    aff(V2("Zi"), V2("Zb"), [[16, 9], [0, 16]], A.is_ge, 4, -1)
 
     def Z(name, i):
         return V2(name, 15 - i, 143 - i)
 
+    for z in range(3):
+        act(V2("Vwin", 512 * z, 512 * z + 512), V2("rst"), scale=0.0)
+
+    cp(V2("I1"), V2("Id"))
+    ts(V2("I4"), V2("Id"), 4096.0, None, A.mult)
     cp(V2("rkF", p=P8), V2("rkI", p=P8))
     ts(V2("loI"), V2("sdI"), 4095, None, A.bitwise_and)
     ts(V2("hiI"), V2("sdI"), 12, None, A.arith_shift_right)
@@ -235,8 +246,9 @@ def rank_program(g, core, T, topo):
     ts(V2("Lr"), V2("iotaK"), V2("loF"), None, A.add)
     ts(V2("hpF"), V2("hiI"), 64.0, -262144.0, A.mult, A.add)
     ts(V2("Lq"), V2("Lr"), 4095, None, A.bitwise_and)
+    ts(V2("Hh"), V2("onef", 0, 64), V2("hiF"), -2048.0, A.mult, A.add)
     tt(V2("b6", 0, 64), V2("Lq"), V2("Lq"), A.mult)
-    ts(V2("Vp"), V2("Lq"), 4096.0, V2("hiF"), A.mult, A.add)
+    ts(V2("Lh"), V2("Lq"), -2048.0, None, A.add)
     ts(V2("t1"), V2("b6", 0, 64), V2("hpF"), None, A.add)
     ts(V2("Lp"), V2("Lq"), 64.0, -262144.0, A.mult, A.add)
     ts(V2("Bq"), V2("t1"), 6, 4095, A.arith_shift_right, A.bitwise_and)
@@ -248,18 +260,18 @@ def rank_program(g, core, T, topo):
     ts(V2("w12"), V2("t2"), 3, 28672, A.arith_shift_right, A.bitwise_and)
     tt(V2("Zk"), V2("w12"), V2("Bq"), A.add)
 
-    xb = ["b0", "b1", "b7"]
+    def spread(bank, us):
+        for j, u in enumerate(us):
+            o = V2(bank, 64 * j, 64 * j + 64)
+            mm(o, V2("I4", u, u + 128), V2("Lh"), True, False)
+            mm(o, V2("I1", u, u + 128), V2("Hh"), False, True)
+        for j, u in enumerate(us):
+            act(V2("VxS", u, 1024, 16, key="VxS%d" % u), V2(bank, 64 * j, 64 * j + 64))
 
-    def spread(us):
-        for u in us:
-            mm(V2(xb[u // 2 % 3], 64 * (u % 2), 64 * (u % 2) + 64), V2("IdF", u, u + 128), V2("Vp"), True, True)
-            if u % 2:
-                for w in (u - 1, u):
-                    act(V2("VxS", w, 1024, 16, key="VxS%d" % w), V2(xb[u // 2 % 3], 64 * (w % 2), 64 * (w % 2) + 64))
-
-    act(V2("Id192"), V2("Id"), scale=192.0)
-    spread(range(0, 4))
+    act(V2("Id192"), V2("Id", 0, 128), scale=192.0)
+    spread("b0", range(0, 6))
     own = V2("b3", 0, 64)
+    IdM = V2("Id", 0, 128)
     k = 0
     for w in range(8):
         ts(V2("stp", 64 * k, 64 * k + 64), V2("Zk"), V2("tA", w, w + 1), V2("dA", w, w + 1), A.is_ge, A.mult)
@@ -268,8 +280,9 @@ def rank_program(g, core, T, topo):
             ts(V2("stp", 64 * k, 64 * k + 64), V2("Zk"), 4096.0 * (w + 1), V2("dB", w, w + 1), A.is_ge, A.mult)
             k += 1
     for j in range(15):
-        mm(own, V2("Id"), V2("stp", 64 * j, 64 * j + 64), j == 0, j == 14)
-    spread(range(4, 8))
+        mm(own, IdM, V2("stp", 64 * j, 64 * j + 64), j == 0, j == 14)
+    spread("b1", range(6, 11))
+    spread("b7", range(11, 16))
     for s in range(N):
         ts(V2("b2", 64 * s, 64 * s + 64), own, float(owner[s]), None, A.is_equal)
     op("v", lambda: g.vector.tensor_tensor_scan(T.Pc[:], T.rst[:], T.b2[:], 0.0, A.mult, A.add), [V2("Pc")], [V2("rst"), V2("b2")])
@@ -279,66 +292,86 @@ def rank_program(g, core, T, topo):
     mm(V2("b4", 16, 24), V2("Tri"), cnt, True, True)
     f2 = V2("b5", 0, 64)
     mm(f2, V2("Id192"), V2("ownb"), True, False)
-    spread(range(8, 10))
     for s in range(N):
-        mm(f2, V2("Id"), V2("Dc", 64 * s, 64 * s + 64), False, False)
+        mm(f2, IdM, V2("Dc", 64 * s, 64 * s + 64), False, False)
     for s in range(N):
         ts(V2("Of", 64 * s, 64 * s + 64), V2("ownb"), float(owner[s]), V2("b4", 16 + s, 17 + s), A.is_equal, A.mult)
-        mm(f2, V2("Id"), V2("Of", 64 * s, 64 * s + 64), False, s == N - 1)
-    spread(range(10, 16))
-    for z in range(4):
-        act(V2("W1", 512 * z, 512 * z + 512), V2("rst"), scale=0.0)
+        mm(f2, IdM, V2("Of", 64 * s, 64 * s + 64), False, s == N - 1)
+    ts(V2("ot"), V2("b4", 16, 24), -2.0, 1.0, A.mult, A.add)
+    cp((T.rnS[:, :, 1], [("rnS", 2 * s + 1, 2 * s + 2) for s in range(N)]), cnt)
     ts(V2("F2u"), f2, -1.0, None, A.add)
-
-    ts(V2("T0"), V2("thrI"), 4096.0, None, A.mult)
-    tt(V2("T1"), V2("T0"), V2("aliI"), A.add)
-    ts(V2("T2"), V2("T1"), 16777216.0, None, A.min)
-    cp(V2("p0"), V2("T2"))
-    tt(V2("r1"), V2("T2"), V2("p0"), A.subtract)
-    cp(V2("p1"), V2("r1"))
-    tt(V2("p2"), V2("r1"), V2("p1"), A.subtract)
+    tt((T.rnS[:, :, 0], [("rnS", 2 * s, 2 * s + 1) for s in range(N)]), V2("ot"), cnt, A.subtract)
+    send([(s, owner[s], V3("rnS", s, s + 1, 0, 2), T.rn[:, s, :]) for s in FAR], "rn")
+    aff(V2("Za"), V2("Zs"), [[-16, 9], [0, 16]], A.is_ge, 0, 1)
+    aff(V2("Zt"), V2("Za"), [[16, 9], [0, 16]], A.is_ge, 2, -1)
+    aff(V2("Zs"), V2("Za"), [[16, 9], [0, 16]], A.is_ge, 15, -1)
+    iota(V2("Ci"), [[0, 3], [2048, 3], [0, LC]], 0, 0, True)
+    aff(V2("Zb"), V2("Zs"), [[-16, 9], [0, 16]], A.is_ge, -3, 1)
+    aff(V2("Zi"), V2("Zb"), [[16, 9], [0, 16]], A.is_ge, 4, -1)
 
     vxs = (T.VxS[:], [("VxS%d" % u, u, 1024) for u in range(16)])
     cp(IX(V2("Vwin"), V2("F2u")), vxs)
     for s in range(N):
         q = owner[s]
         dma("ys"[s % 2], V3("vl", s, s + 1, 0, LC), (T.Vwin[0:128:16, CAPQ * q:CAPQ * q + CAPQ], [("Vwin", CAPQ * q, CAPQ * q + CAPQ)]))
-    for z in range(4):
-        act(V2("IDx", 432 * z, 432 * z + 432), V2("rst", 0, 432), scale=0.0)
 
-    ts((T.msg[:, :, 49], [("msg", MW * s + 49, MW * s + 50) for s in range(N)]), cnt, 1.0, None, A.mult)
-    ts(V2("ot"), V2("b4", 16, 24), -2.0, 1.0, A.mult, A.add)
-    tt((T.msg[:, :, 48], [("msg", MW * s + 48, MW * s + 49) for s in range(N)]), V2("ot"), cnt, A.subtract)
-    ts(V2("eW"), V2("eIo"), 2047, None, A.bitwise_and)
-    cp(V2("p3"), V2("eW"))
-    tt(V2("p4"), V2("eW"), V2("p3"), A.subtract)
-    for j in range(5):
-        need("y", [], [("W1", 0, 2048)])
-        dma("y", (T.W1[j:128:16, :], [("W1p%d" % j, 0, 2048)]), V2("p%d" % j))
-    tab = (T.W1[:], [("W1", 0, 2048)] + [("W1p%d" % j, 0, 2048) for j in range(5)])
+    def piece(j):
+        dma("y", (T.W1[j:128:16, :], [("W1p%d" % j, 0, 2048)]), V2("p%d" % j), [("W1", 0, 2048)])
+
+    def pieces():
+        piece(4)
+        ts(V2("T0"), V2("thrI"), 4096.0, None, A.mult)
+        tt(V2("T1"), V2("T0"), V2("aliI"), A.add)
+        ts(V2("T2"), V2("T1"), 16777216.0, None, A.min)
+        cp(V2("p0"), V2("T2"))
+        tt(V2("r1"), V2("T2"), V2("p0"), A.subtract)
+        cp(V2("p1"), V2("r1"))
+        tt(V2("p2"), V2("r1"), V2("p1"), A.subtract)
+        for j in range(3):
+            piece(j)
+    tab = (T.W1[:], [("W1", 0, 2048)] + [("W1p%d" % j, 0, 2048) for j in (0, 1, 2, 4)])
+
+    def RN(s, k):
+        return V3("rnS" if s == S0 else "rn", s, s + 1, k, k + 1)
+
+    order = [s for c in CH for s in range(*c)]
+    for s in order:
+        act(V2("ab", CAPQ * s, CAPQ * s + CAPQ), V2("jc"), F.Abs, bias=RN(s, 0))
+
+    def masks(a, b):
+        for s in order[a:b]:
+            ts(V2("mk", CAPQ * s, CAPQ * s + CAPQ), V2("ab", CAPQ * s, CAPQ * s + CAPQ), RN(s, 1), float(2 ** (20 - asker[s])), A.is_lt, A.mult)
 
     def ylist():
         ts(V2("F2i"), f2, -1.0, None, A.add)
-        ts(V2("own200"), V2("ownb"), 200.0, None, A.mult)
+        ts(V2("own176"), V2("ownb"), 176.0, None, A.mult)
         ts(V2("own2k"), V2("ownb"), 2048.0, None, A.mult)
         ts(V2("ya"), V2("F2i"), 10923.0, None, A.mult)
         ts(V2("yc"), V2("F2i"), 16.0, None, A.mult)
         ts(V2("yb"), V2("ya"), 17, None, A.arith_shift_right)
-        tt(V2("yc"), V2("yc"), V2("own200"), A.add)
+        tt(V2("yc"), V2("yc"), V2("own176"), A.add)
         ts(V2("yb"), V2("yb"), -191.0, None, A.mult)
         tt(V2("yd"), V2("yb"), V2("yc"), A.add)
         cp(V2("yo"), V2("yd"))
 
-    def hashes(a, b):
+    def hashes(c):
+        a, b = HS[c]
+
         def W(nm):
             return V3(nm, a, b, 0, 48)
-        for i in range(4):
+
+        def out(sem, src, dst):
+            for gr in GRP:
+                if a <= gr[0] < b:
+                    send([(s, owner[s], src(s), dst(s)) for s in gr], sem)
+        e = b if c == 0 else N
+        for i in range(4 if c < 2 else 0):
             kk = ((1597 * (i + 1)) & 4095) - 4096
-            ts(V3("hx", a, b, LC * i, LC * i + LC), V3("vl", a, b, 0, LC), 4096.0 * kk, None, A.add)
+            ts(V3("hx", a, e, LC * i, LC * i + LC), V3("vl", a, e, 0, LC), 4096.0 * kk + 2048.0 * 4097.0, None, A.add)
         ts(W("hL"), W("hx"), 12, 4095, A.arith_shift_right, A.bitwise_and)
         ts(W("h4"), W("hx"), 4095, None, A.bitwise_and)
         tt(W("hq"), W("hL"), W("hL"), A.mult)
-        p = V2("b6", 0, 48 * (b - a))
+        p = V2("b6", 48 * a, 48 * b)
         ts(p, W("h4"), 64.0, -262144.0, A.mult, A.add)
         tt(W("ht"), W("hq"), p, A.add)
         ts(p, W("hL"), 64.0, -262144.0, A.mult, A.add)
@@ -347,98 +380,94 @@ def rank_program(g, core, T, topo):
         tt(W("hu"), W("hb"), p, A.add)
         ts(p, W("hB"), 4096.0, 2048.0, A.mult, A.add)
         ts(W("he"), W("hu"), 7, 2047, A.arith_shift_right, A.bitwise_and)
+        cp(V2("le", 48 * a, 48 * b), W("he"))
+        out("rl", lambda s: V2("le", 48 * s, 48 * s + 48), lambda s: T.rl[:, 48 * s:48 * s + 48])
         tt(W("msg"), W("he"), p, A.add)
-        for gr in GRP:
-            if a <= gr[0] < b:
-                send([(s, owner[s], V3("msg", s, s + 1, 0, 50), T.rq[:, s, 0:50]) for s in gr], "rq")
+        out("rq", lambda s: V3("msg", s, s + 1, 0, 48), lambda s: T.rq[:, s, :])
+
+    def look(c):
+        a, b = CH[c]
+        lst = "le" if a == S0 else "rl"
+        for s in range(a, b):
+            act(V2("GT", 768 * s, 768 * s + 768), IX(tab, V2(lst, 48 * s, 48 * s + 48)))
 
     def arrive(c):
         a, b = CH[c]
-        if a <= S0 < b:
-            cp(V3("rq", S0, S0 + 1, 0, 50), V3("msg", S0, S0 + 1, 0, 50))
-        ts(V3("eI", a, b, 0, 48), V3("rq", a, b, 0, 48), 2047, None, A.bitwise_and)
-        cp(V2("le", 48 * a, 48 * b), V3("eI", a, b, 0, 48))
-        cp(V2("nbh", 2 * a, 2 * b), V3("rq", a, b, 48, 50))
-        act(V2("GT", 768 * a, 768 * b), IX(tab, V2("le", 48 * a, 48 * b)))
-        for s in range(a, b):
-            act(V2("ab", CAPQ * s, CAPQ * s + CAPQ), V2("jc"), F.Abs, bias=V2("nbh", 2 * s, 2 * s + 1))
         for i in range(16):
-            mm(V2("b%d" % (c % 2), 0, 48 * (b - a)), Z("Zt", i), V2("GT", 768 * a + i, 768 * b, 16), i == 0, i == 15)
+            mm(V2(TB[c % 3], 0, 48 * (b - a)), Z("Zt", i), V2("GT", 768 * a + i, 768 * b, 16), i == 0, i == 15)
 
     def filt(c):
         a, b = CH[c]
-        n = LC * (b - a)
-        tt(V3("mn", a, b, 0, 48), V3("rq", a, b, 0, 48), V2("b%d" % (c % 2), 0, 4 * n), A.min)
+        tt(V3("mn", a, b, 0, 48), V3("msg" if a == S0 else "rq", a, b, 0, 48), V2(TB[c % 3], 0, 48 * (b - a)), A.min)
         ts(V3("cI", a, b, 0, 48), V3("mn", a, b, 0, 48), 2047, None, A.bitwise_and)
+        cp(V2("ls", 36 * a, 36 * b), V3("cI", a, b, 0, 36))
         for s in range(a, b):
-            ts(V2("mk", CAPQ * s, CAPQ * s + CAPQ), V2("ab", CAPQ * s, CAPQ * s + CAPQ), V2("nbh", 2 * s + 1, 2 * s + 2), float(2 ** (14 - asker[s])), A.is_lt, A.mult)
-
-        def L(i):
-            return V2("ls", 36 * a + n * i, 36 * a + n * i + n)
-        for i in range(3):
-            cp(L(i), V3("cI", a, b, LC * i, LC * i + LC))
-        for i in range(3):
-            o = 576 * a + 16 * n * i
-            tt(V2("MG", o, o + 16 * n), IX(V2("seenS"), L(i)), V2("mk", CAPQ * a, CAPQ * b), A.mult)
+            for i in range(3):
+                o = 576 * s + CAPQ * i
+                tt(V2("MG", o, o + CAPQ), IX(V2("seenS"), V2("ls", 36 * s + LC * i, 36 * s + LC * i + LC)), V2("mk", CAPQ * s, CAPQ * s + CAPQ), A.mult)
+        o = V2("b%d" % (2 + c % 2), 0, 36 * (b - a))
+        mm(o, IdM, V2("Ci", 0, 36 * (b - a)), True, False)
         for i in range(16):
-            mm(V2("b%d" % (2 + c % 2), 0, 3 * n), Z("Zs", i), V2("MG", 576 * a + i, 576 * b, 16), i == 0, i == 15)
-        for i in range(4):
-            ts(V2("b7", 48 * a + n * i, 48 * a + n * i + n), V3("cI", a, b, LC * i, LC * i + LC), 2048.0 * i, None, A.add)
+            mm(o, Z("Zs", i), V2("MG", 576 * a + i, 576 * b, 16), False, i == 15)
+        ts(V3("ky", a, b, 36, 48), V3("cI", a, b, 36, 48), 6144.0, None, A.add)
 
     def pick(c):
         a, b = CH[c]
-        n = LC * (b - a)
-        h, o = (36 * a, 36 * b), 48 * a
-        cp(V2("sI", *h), V2("b%d" % (2 + c % 2), 0, 3 * n))
-        ts(V2("sb", *h), V2("sI", *h), 16384, None, A.bitwise_and)
-        tt(V2("ky", *h), V2("sb", *h), V2("b7", o, o + 3 * n), A.add)
-        x, h = (LC * a, LC * b), 36 * a
-        tt(V2("ka", *x), V2("ky", h, h + n), V2("ky", h + n, h + 2 * n), A.min)
-        tt(V2("kb", *x), V2("ky", h + 2 * n, h + 3 * n), V2("b7", o + 3 * n, o + 4 * n), A.min)
-        tt(V2("kc", *x), V2("ka", *x), V2("kb", *x), A.min)
+        cp(V2("sI", 36 * a, 36 * b), V2("b%d" % (2 + c % 2), 0, 36 * (b - a)))
+        ts(V3("sb", a, b, 0, 36), V2("sI", 36 * a, 36 * b), 2 ** 20 + 3 * 2048, None, A.bitwise_and)
+        tt(V3("ky", a, b, 0, 36), V3("sb", a, b, 0, 36), V3("cI", a, b, 0, 36), A.add)
+        tt(V3("m2", a, b, 0, 24), V3("ky", a, b, 0, 24), V3("ky", a, b, 24, 48), A.min)
+        x = (LC * a, LC * b)
+        tt(V2("kc", *x), V3("m2", a, b, 0, 12), V3("m2", a, b, 12, 24), A.min)
         ts(V2("xI", *x), V2("kc", *x), 2047, None, A.bitwise_and)
         cp(V2("lx", *x), V2("xI", *x))
-        for s in range(a, b):
-            R = V2("land", RW * me, RW * me + 192) if s == S0 else V3("rs", s, s + 1, 0, 192)
-            act(R, IX(V2("vecS"), V2("lx", LC * s, LC * s + LC)))
-        for (u, w) in ([(a, S0), (S0, S0 + 1), (S0 + 1, b)] if a <= S0 < b else [(a, b)]):
-            if u < w:
-                hi = V2("land", RW * me + 192, RW * me + 204) if u == S0 else V3("rs", u, w, 192, 204)
-                lo = V2("land", RW * me + 204, RW * me + 216) if u == S0 else V3("rs", u, w, 204, 216)
-                xs = V2("xI", LC * u, LC * w)
-                cp(hi, xs)
-                tt(lo, xs, hi, A.subtract)
+        if a == S0:
+            act(V2("land", CAPQ * me, CAPQ * me + CAPQ), IX(V2("vecS"), V2("lx", *x)))
+            return
+        act(V2("rs", CAPQ * a, CAPQ * b), IX(V2("vecS"), V2("lx", *x)))
         for gr in GRP:
             if a <= gr[0] < b:
-                send([(s, asker[s], V3("rs", s, s + 1, 0, RW), T.land[:, RW * me:RW * me + RW]) for s in gr], "la")
+                send([(s, asker[s], V2("lx", LC * s, LC * s + LC), T.lr[:, LC * s:LC * s + LC]) for s in gr], "lr")
+                send([(s, asker[s], V2("rs", CAPQ * s, CAPQ * s + CAPQ), T.land[:, CAPQ * me:CAPQ * me + CAPQ]) for s in gr], "la")
 
     def items(c):
-        a, b = CH[c]
-        for s in range(a, b):
-            o = RW * owner[s]
-            tt(V2("xf", LC * s, LC * s + LC), V2("land", o + 192, o + 204), V2("land", o + 204, o + 216), A.add)
-        cp(V2("xu", LC * a, LC * b), V2("xf", LC * a, LC * b))
-        for s in range(a, b):
-            o = RW * owner[s]
-            act(V2("IDx", o, o + 192), IX(tab, V2("xu", LC * s, LC * s + LC)))
+        for s in range(*CH[c]):
+            o = CAPQ * owner[s]
+            act(V2("IDx", o, o + CAPQ), IX(tab, V2("lx" if s == S0 else "lr", LC * s, LC * s + LC)))
 
-    for (f, *x) in PLAN:
-        {"H": hashes, "A": arrive, "F": filt, "P": pick, "I": items, "Y": ylist}[f](*x)
+    BLOCK = {"H": hashes, "G": look, "A": arrive, "F": filt, "P": pick, "I": items, "Y": ylist, "M": masks, "T": pieces}
+    for x in PLAN:
+        x = x if isinstance(x, list) else [x]
+        rows = []
+        for (f, *y) in x:
+            stream[0] = []
+            BLOCK[f](*y)
+            row = [[]]
+            for (q, h) in stream[0]:
+                if q == "v" and row[-1]:
+                    row.append([])
+                row[-1].append(h)
+            rows.append([[]] * (4 if f == "P" and len(x) > 1 else 0) + row)
+        stream[0] = None
+        for k in range(max(len(row) for row in rows)):
+            for row in rows:
+                for h in (row[k] if k < len(row) else []):
+                    h()
 
     def ygat(h):
         return V2("yS", 512 * h, 512 * h + 512), IX(V2("land"), V2("yo", 32 * h, 32 * h + 32))
 
     def igat(h):
         return V2("IDg", 512 * h, 512 * h + 512), IX(V2("IDx"), V2("yo", 32 * h, 32 * h + 32))
+    act(*igat(1))
+    cp(*igat(0))
     cp(*ygat(0))
     dma("y", hbm(T.y[:, 0:512]), V2("yS", 0, 512))
-    act(*igat(0))
-    cp(*igat(1))
     act(*ygat(1))
-    dma("y", hbm(T.y[:, 512:1024]), V2("yS", 512, 1024))
     for i in range(16):
         mm(V2("b4", 64, 128), Z("Zi", i), V2("IDg", i, 1024, 16), i == 0, i == 15)
     tt(V2("chS"), V2("own2k"), V2("b4", 64, 128), A.add)
+    dma("s", hbm(T.y[:, 512:1024]), V2("yS", 512, 1024))
     dma("s", hbm(T.chosen[:]), V2("chS"))
 
     for s, n in count.items():

@@ -4,13 +4,15 @@ from concourse.mybir import AluOpType, ActivationFunctionType
 A = AluOpType
 F = ActivationFunctionType
 N = 8
-DIST = [1, 3, 0, 5, 7, 2, 4, 6]
 CAPQ, LC = 192, 12
-HS = [(0, 2), (2, 5), (5, 8)]
-CH = [(2, 3), (0, 2), (3, 5), (5, 7), (7, 8)]
-GRP = [(0, 1), (3, 4), (5, 6), (7,)]
-PLAN = [[("T",), ("Y",)], ("H", 0), ("H", 1), ("G", 0), ("A", 0), ("G", 1), [("H", 2), ("M", 0, 8)], ("A", 1), ("G", 2), ("F", 0), ("G", 3), ("A", 2), [("F", 1), ("P", 0)],
-        ("A", 3), [("F", 2), ("P", 1)], ("G", 4), ("A", 4), ("I", 0), [("F", 3), ("P", 2)], [("F", 4), ("P", 3)], ("P", 4), ("I", 1), ("I", 2), ("I", 3), ("I", 4)]
+S0 = N - 1
+HS = [(0, 2), (2, 4), (4, 8)]
+CH = [(0, 2), (2, 4), (4, 6), (6, 7), (7, 8)]
+GRP = [(0, 1), (2, 3), (4, 5), (6,)]
+PLAN = [[(0, "T")],
+        [(0, "H", 0), (7, "H", 1), (24, "G", 0), (24, "A", 0), (25, "G", 1), (20, "H", 2), (22, "M", 0, 4), (34, "A", 1), (34, "G", 2)],
+        [(0, "F", 0), (0, "M", 4, 8), (1, "G", 3), (9, "A", 2), (8, "F", 1), (13, "P", 0), (17, "A", 3), (20, "G", 4), (16, "F", 2), (21, "P", 1), (25, "A", 4),
+         (24, "F", 3), (27, "P", 2), (34, "I", 0), (30, "F", 4), (33, "P", 3), (40, "I", 1), (40, "P", 4), (39, "Y"), (52, "I", 4), (53, "I", 2), (54, "I", 3)]]
 TB = ["b0", "b1", "b7"]
 f32, b16, i32, u16, f16 = "float32", "bfloat16", "int32", "uint16", "float16"
 SHAPES = {
@@ -182,9 +184,13 @@ def rank_program(g, core, T, topo):
     def send(pairs, sem):
         later("g", lambda: send_now(pairs, sem))
 
-    owner = [(me + d) % N for d in DIST]
-    asker = [(me - d) % N for d in DIST]
-    S0 = DIST.index(0)
+    def hops(d):
+        a, b = topo.chip(T.cores[0]), topo.chip(T.cores[d])
+        return 3 if d == 0 else 2 if topo.mates(a, b) else 1 if topo.same_plane(a, b) else 0
+
+    DIST = sorted(range(N), key=hops)
+    owner = [me ^ d for d in DIST]
+    asker = owner
     FAR = [s for s in range(N) if s != S0]
 
     def arrives(sem, s, src, view, together):
@@ -334,12 +340,11 @@ def rank_program(g, core, T, topo):
     def RN(s, k):
         return V3("rnS" if s == S0 else "rn", s, s + 1, k, k + 1)
 
-    order = [s for c in CH for s in range(*c)]
-    for s in order:
+    for s in range(N):
         act(V2("ab", CAPQ * s, CAPQ * s + CAPQ), V2("jc"), F.Abs, bias=RN(s, 0))
 
     def masks(a, b):
-        for s in order[a:b]:
+        for s in range(a, b):
             ts(V2("mk", CAPQ * s, CAPQ * s + CAPQ), V2("ab", CAPQ * s, CAPQ * s + CAPQ), RN(s, 1), float(2 ** (20 - asker[s])), A.is_lt, A.mult)
 
     def ylist():
@@ -436,23 +441,19 @@ def rank_program(g, core, T, topo):
             act(V2("IDx", o, o + CAPQ), IX(tab, V2("lx" if s == S0 else "lr", LC * s, LC * s + LC)))
 
     BLOCK = {"H": hashes, "G": look, "A": arrive, "F": filt, "P": pick, "I": items, "Y": ylist, "M": masks, "T": pieces}
-    for x in PLAN:
-        x = x if isinstance(x, list) else [x]
-        rows = []
-        for (f, *y) in x:
+    for blocks in PLAN:
+        turns = []
+        for n, (k, f, *y) in enumerate(blocks):
             stream[0] = []
             BLOCK[f](*y)
-            row = [[]]
+            started = False
             for (q, h) in stream[0]:
-                if q == "v" and row[-1]:
-                    row.append([])
-                row[-1].append(h)
-            rows.append([[]] * (4 if f == "P" and len(x) > 1 else 0) + row)
+                k += 1 if q == "v" and started else 0
+                started = True
+                turns.append((k, n, len(turns), h))
         stream[0] = None
-        for k in range(max(len(row) for row in rows)):
-            for row in rows:
-                for h in (row[k] if k < len(row) else []):
-                    h()
+        for x in sorted(turns, key=lambda x: x[:3]):
+            x[3]()
 
     def ygat(h):
         return V2("yS", 512 * h, 512 * h + 512), IX(V2("land"), V2("yo", 32 * h, 32 * h + 32))

from concourse.bass import DstId, RemoteDMATransfer
from concourse.mybir import AluOpType, ActivationFunctionType

A = AluOpType
F = ActivationFunctionType
N = 8
CAPQ, LC = 192, 12
S0 = N - 1
HS = [(0, 2), (2, 4), (4, 8)]
CH = [(0, 2), (2, 4), (4, 6), (6, 7), (7, 8)]
GRP = [(0, 1), (2, 3), (4, 5), (6,)]
PLAN = [[(0, "T")],
        [(0, "H", 0), (7, "H", 1), (24, "G", 0), (24, "A", 0), (25, "G", 1), (20, "H", 2), (22, "M", 0, 4), (34, "A", 1), (34, "G", 2)],
        [(0, "F", 0), (0, "M", 4, 8), (1, "G", 3), (9, "A", 2), (8, "F", 1), (13, "P", 0), (17, "A", 3), (20, "G", 4), (16, "F", 2), (21, "P", 1), (25, "A", 4),
         (24, "F", 3), (27, "P", 2), (34, "I", 0), (30, "F", 4), (33, "P", 3), (40, "I", 1), (40, "P", 4), (39, "Y"), (52, "I", 4), (53, "I", 2), (54, "I", 3)]]
TB = ["b0", "b1", "b7"]
f32, b16, i32, u16, f16 = "float32", "bfloat16", "int32", "uint16", "float16"
SHAPES = {
    i32: {"sdI": 1, "rkI": 16, "thrI": 128, "aliI": 128, "iotaK": 64,
          "loI": 1, "hiI": 1, "Lr": 64, "Lq": 64, "t1": 64, "Bq": 64, "Lp": 64, "t2": 64, "w12": 64,
          "F2i": 64, "ya": 64, "yb": 64, "yc": 64, "yd": 64, "own176": 64,
          "hx": (8, 48), "hL": (8, 48), "h4": (8, 48), "hq": (8, 48), "ht": (8, 48), "hB": (8, 48), "hb": (8, 48), "hu": (8, 48), "he": (8, 48),
          "mn": (8, 48), "cI": (8, 48), "sI": 288, "sb": (8, 36), "ky": (8, 48), "m2": (8, 24), "kc": 96, "xI": 96},
    f32: {"rkF": 16, "onef": 128, "Rm": 128, "w1c": 8, "w4c": 8, "loF": 1, "hiF": 1, "hpF": 1, "Zk": 64, "tA": 8, "dA": 8, "dB": 8,
          "VxS": 1024, "Vwin": 1536, "vl": (8, 12), "own2k": 64, "ot": 8, "T0": 128, "T1": 128, "T2": 128, "r1": 128,
          "rnS": (8, 2), "rn": (8, 2), "msg": (8, 48), "rq": (8, 48), "chS": 64},
    b16: {"seenS": 2048, "vecS": 2048, "W1": 2048, "oneb": 144, "Id": 144, "Id192": 128, "Tri": 128, "rst": 512, "Ci": 108,
          "Zs": 144, "Za": 144, "Zb": 144, "Zt": 144, "Zi": 144, "jc": 192, "stp": 1024, "Pc": 512, "Dc": 512, "Of": 512, "ownb": 64,
          "p0": 128, "p1": 128, "p2": 128, "p4": 128, "rs": 1536, "land": 1536, "ab": 1536, "mk": 1536, "GT": 6144, "MG": 4608,
          "IDx": 1536, "IDg": 1024, "yS": 1024},
    u16: {"F2u": 64, "yo": 64, "le": 384, "rl": 384, "lx": 96, "lr": 96, "ls": 288},
    f16: {"I1": 144, "I4": 144, "Lh": 64, "Hh": 64},
}
SCRATCH = {}
for _dt, _d in SHAPES.items():
    for _k, _n in _d.items():
        SCRATCH[_k] = ("sbuf", [128] + (list(_n) if isinstance(_n, tuple) else [_n]), _dt)
for _b in range(8):
    SCRATCH["b%d" % _b] = ("psum", [128, 512], f32)
SEMAPHORES = ["sv", "ss", "st", "sg", "lsem"] + ["d%d" % _k for _k in range(32)] + ["%s%d" % (_m, _k) for _m in ("rn", "rl", "rq", "lr", "la") for _k in range(N)]


def rank_program(g, core, T, topo):
    me = T.rank_of(core)
    if me is None:
        return
    queue = {"v": g.vector, "s": g.scalar, "t": g.tensor, "g": g, "y": g.sync}
    count = {}
    clock = {q: {} for q in queue}
    seen_by = {}
    log = {}
    ndma = [0]

    def V2(name, a=0, b=None, step=1, p=None, key=None):
        b = SCRATCH[name][1][1] if b is None else b
        ap = T[name][:, a:b:step] if p is None else T[name][p, a:b:step]
        return (ap, [(key or name, a, b)])

    def V3(name, s0, s1, a, b):
        w = SCRATCH[name][1][2]
        ap = T[name][:, s0, a:b] if s1 == s0 + 1 else T[name][:, s0:s1, a:b]
        return (ap, [(name, s * w + a, s * w + b) for s in range(s0, s1)])

    def IX(win, off):
        return (win[0].indirect(off[0]), win[1] + off[1])

    BANKS = ["b%d" % k for k in range(8)]

    def need(q, reads, writes):
        toks = []
        for regs, w in ((reads, False), (writes, True)):
            for (k, lo, hi) in regs:
                for (l2, h2, w2, tok, e2) in log.get(k, []):
                    if k in BANKS and e2 != q:
                        toks.append(tok)
                    elif l2 < hi and lo < h2 and (w or w2) and not (q == "t" and e2 == "t"):
                        toks.append(tok)
        best = {}
        for (s, n) in toks:
            if clock[q].get(s, 0) < n:
                best[s] = max(best.get(s, 0), n)
        for s in sorted(best, key=lambda s: (s[0] != "d", s)):
            n = best[s]
            if clock[q].get(s, 0) < n:
                queue[q].wait_ge(T.sem[s], n)
                clock[q][s] = n
                for s2, n2 in seen_by.get((s, n), {}).items():
                    clock[q][s2] = max(clock[q].get(s2, 0), n2)

    def done(q, inst, reads, writes, sem, inc):
        inst.then_inc(T.sem[sem], inc)
        count[sem] = count.get(sem, 0) + inc
        tok = (sem, count[sem])
        c = dict(clock[q])
        c[sem] = count[sem]
        seen_by[tok] = c
        for regs, w in ((reads, False), (writes, True)):
            for (k, lo, hi) in regs:
                log.setdefault(k, []).append((lo, hi, w, tok, q))

    stream = [None]

    def later(q, f):
        if stream[0] is None:
            f()
        else:
            stream[0].append((q, f))

    def now(q, f, outs, ins):
        reads = [r for x in ins for r in x[1]]
        writes = [r for x in outs for r in x[1]]
        need(q, reads, writes)
        done(q, f(), reads, writes, "s" + q, 1)

    def op(q, f, outs, ins):
        later(q, lambda: now(q, f, outs, ins))

    def isv(x):
        return isinstance(x, tuple)

    def raw(x):
        return x[0] if isv(x) else x

    def ts(out, in0, s1, s2, o0, o1=None):
        ins = [x for x in (in0, s1, s2) if isv(x)]
        if o1 is None:
            op("v", lambda: g.vector.tensor_scalar(out[0], in0[0], raw(s1), None, o0), [out], ins)
        else:
            op("v", lambda: g.vector.tensor_scalar(out[0], in0[0], raw(s1), raw(s2), o0, o1), [out], ins)

    def tt(out, a, b, o):
        op("v", lambda: g.vector.tensor_tensor(out[0], a[0], b[0], o), [out], [a, b])

    def cp(out, a):
        op("v", lambda: g.vector.tensor_copy(out[0], a[0]), [out], [a])

    def fill(out, c):
        op("v", lambda: g.vector.memset(out[0], c), [out], [])

    def act(out, a, func=F.Copy, **kw):
        ins = [a] + [x for x in kw.values() if isv(x)]
        k2 = {k: raw(x) for k, x in kw.items()}
        op("s", lambda: g.scalar.activation(out[0], a[0], func, **k2), [out], ins)

    def mm(out, lhs, rhs, start, stop):
        op("t", lambda: g.tensor.matmul(out[0], lhs[0], rhs[0], start, stop), [out], [lhs, rhs])

    def aff(out, a, pat, cmp, base, cm):
        op("g", lambda: g.affine_select(out[0], a[0], pat, cmp, 0.0, base, cm), [out], [a])

    def iota(out, pat, base, cm, small=False):
        if small:
            op("g", lambda: g.iota(out[0], pat, base, cm, allow_small_or_imprecise_dtypes=True), [out], [])
        else:
            op("g", lambda: g.iota(out[0], pat, base, cm), [out], [])

    def dma_now(q, out, a, after):
        need(q, a[1], out[1] + after)
        sem = "d%d" % ndma[0]
        ndma[0] += 1
        done(q, queue[q].dma_start(out[0], a[0]), a[1], out[1], sem, 16)

    def dma(q, out, a, after=()):
        later(q, lambda: dma_now(q, out, a, list(after)))

    def hbm(ap):
        return (ap, [])

    def send_now(pairs, sem):
        need("g", [r for x in pairs for r in x[2][1]], [])
        tr = []
        for j, (s, q, a, o) in enumerate(pairs):
            eng = topo.engines(core, T.cores[q])
            n = len(eng) // len(pairs)
            rid, pid, se = topo.addr(T.cores[q])
            count["lsem"] = count.get("lsem", 0) + n
            if len(pairs) == 1:
                g.remote_dma(o, a[0], T.sem["%s%d" % (sem, s)], T.sem.lsem, pid, rid, topo.mask(core, T.cores[q]))
                return
            tr.append(RemoteDMATransfer(dst_ids=[DstId(rid=rid, pnc=pid)], dma_engine_mask=sum(1 << e for e in eng[n * j:n * j + n]),
                                        remote_sem=T.sem["%s%d" % (sem, s)], src=a[0], dst=o))
        g.remote_dma_fused(tr, local_sem=T.sem.lsem)

    def send(pairs, sem):
        later("g", lambda: send_now(pairs, sem))

    def hops(d):
        a, b = topo.chip(T.cores[0]), topo.chip(T.cores[d])
        return 3 if d == 0 else 2 if topo.mates(a, b) else 1 if topo.same_plane(a, b) else 0

    DIST = sorted(range(N), key=hops)
    owner = [me ^ d for d in DIST]
    asker = owner
    FAR = [s for s in range(N) if s != S0]

    def arrives(sem, s, src, view, together):
        n = len(topo.engines(T.cores[src], core)) // together
        name = "%s%d" % (sem, s)
        count[name] = n
        seen_by[(name, n)] = {name: n}
        for (k, lo, hi) in view[1]:
            log.setdefault(k, []).append((lo, hi, True, (name, n), "remote"))

    for s in FAR:
        k = [len(gr) for gr in GRP if s in gr][0]
        arrives("rn", s, asker[s], V3("rn", s, s + 1, 0, 2), N - 1)
        arrives("rl", s, asker[s], V2("rl", 48 * s, 48 * s + 48), k)
        arrives("rq", s, asker[s], V3("rq", s, s + 1, 0, 48), k)
        arrives("lr", s, owner[s], V2("lr", LC * s, LC * s + LC), k)
        arrives("la", s, owner[s], V2("land", CAPQ * owner[s], CAPQ * owner[s] + CAPQ), k)

    dma("y", V2("sdI"), hbm(T.sd[:]))
    dma("s", V2("rkI", p=slice(0, 8)), hbm(T.rk[:]))
    dma("y", V2("thrI"), hbm(T.thr[:]))
    dma("s", V2("aliI"), hbm(T.ali[:]))
    dma("y", V2("seenS"), hbm(T.seen[:]))
    dma("y", V2("vecS"), hbm(T.vec[:]))

    fill(V2("oneb"), 1.0)
    fill(V2("onef"), 1.0)
    fill(V2("rst"), 1.0)
    fill(V2("rst", 0, 512, 64), 0.0)
    fill(V2("Zs"), 0.0)
    fill(V2("Zs", 15, 144, 16), 1.0)
    iota(V2("iotaK"), [[7985, 64]], 0, 0)
    iota(V2("w1c"), [[1, 8]], 0, 0, True)
    iota(V2("w4c"), [[4096, 8]], 0, 0, True)
    P8 = slice(0, 8)
    aff(V2("Id"), V2("oneb"), [[-1, 144]], A.is_equal, 0, 1)
    aff(V2("Rm", p=P8), V2("onef", 0, 128, p=P8), [[1, 128]], A.is_ge, 0, -16)
    aff(V2("Rm", p=P8), V2("Rm", p=P8), [[-1, 128]], A.is_ge, 15, 16)
    aff(V2("Tri"), V2("oneb", 0, 128), [[16, 8], [1, 16]], A.is_gt, 0, -1)
    aff(V2("Tri"), V2("Tri"), [[-16, 8], [0, 16]], A.is_ge, 0, 1)
    iota(V2("W1"), [[128, 16], [0, 128]], 0, 0, True)
    iota(V2("p4"), [[1, 128]], 0, 0, True)
    iota(V2("jc"), [[2, LC], [2 * LC, 16]], 0, 0, True)

    def Z(name, i):
        return V2(name, 15 - i, 143 - i)

    for z in range(3):
        act(V2("Vwin", 512 * z, 512 * z + 512), V2("rst"), scale=0.0)

    cp(V2("I1"), V2("Id"))
    ts(V2("I4"), V2("Id"), 4096.0, None, A.mult)
    cp(V2("rkF", p=P8), V2("rkI", p=P8))
    ts(V2("loI"), V2("sdI"), 4095, None, A.bitwise_and)
    ts(V2("hiI"), V2("sdI"), 12, None, A.arith_shift_right)
    mm(V2("b4", 0, 16), V2("Rm", p=P8), V2("rkF", p=P8), True, True)
    cp(V2("loF"), V2("loI"))
    cp(V2("hiF"), V2("hiI"))
    ts(V2("Lr"), V2("iotaK"), V2("loF"), None, A.add)
    ts(V2("hpF"), V2("hiI"), 64.0, -262144.0, A.mult, A.add)
    ts(V2("Lq"), V2("Lr"), 4095, None, A.bitwise_and)
    ts(V2("Hh"), V2("onef", 0, 64), V2("hiF"), -2048.0, A.mult, A.add)
    tt(V2("b6", 0, 64), V2("Lq"), V2("Lq"), A.mult)
    ts(V2("Lh"), V2("Lq"), -2048.0, None, A.add)
    ts(V2("t1"), V2("b6", 0, 64), V2("hpF"), None, A.add)
    ts(V2("Lp"), V2("Lq"), 64.0, -262144.0, A.mult, A.add)
    ts(V2("Bq"), V2("t1"), 6, 4095, A.arith_shift_right, A.bitwise_and)
    tt(V2("tA"), V2("w4c"), V2("b4", 0, 8), A.add)
    tt(V2("b6", 64, 128), V2("Bq"), V2("Bq"), A.mult)
    tt(V2("dA"), V2("b4", 8, 16), V2("w1c"), A.subtract)
    tt(V2("t2"), V2("Lp"), V2("b6", 64, 128), A.add)
    ts(V2("dB"), V2("dA"), -1.0, 1.0, A.mult, A.add)
    ts(V2("w12"), V2("t2"), 3, 28672, A.arith_shift_right, A.bitwise_and)
    tt(V2("Zk"), V2("w12"), V2("Bq"), A.add)

    def spread(bank, us):
        for j, u in enumerate(us):
            o = V2(bank, 64 * j, 64 * j + 64)
            mm(o, V2("I4", u, u + 128), V2("Lh"), True, False)
            mm(o, V2("I1", u, u + 128), V2("Hh"), False, True)
        for j, u in enumerate(us):
            act(V2("VxS", u, 1024, 16, key="VxS%d" % u), V2(bank, 64 * j, 64 * j + 64))

    act(V2("Id192"), V2("Id", 0, 128), scale=192.0)
    spread("b0", range(0, 6))
    own = V2("b3", 0, 64)
    IdM = V2("Id", 0, 128)
    k = 0
    for w in range(8):
        ts(V2("stp", 64 * k, 64 * k + 64), V2("Zk"), V2("tA", w, w + 1), V2("dA", w, w + 1), A.is_ge, A.mult)
        k += 1
        if w < 7:
            ts(V2("stp", 64 * k, 64 * k + 64), V2("Zk"), 4096.0 * (w + 1), V2("dB", w, w + 1), A.is_ge, A.mult)
            k += 1
    for j in range(15):
        mm(own, IdM, V2("stp", 64 * j, 64 * j + 64), j == 0, j == 14)
    spread("b1", range(6, 11))
    spread("b7", range(11, 16))
    for s in range(N):
        ts(V2("b2", 64 * s, 64 * s + 64), own, float(owner[s]), None, A.is_equal)
    op("v", lambda: g.vector.tensor_tensor_scan(T.Pc[:], T.rst[:], T.b2[:], 0.0, A.mult, A.add), [V2("Pc")], [V2("rst"), V2("b2")])
    cp(V2("ownb"), own)
    tt(V2("Dc"), V2("Pc"), V2("b2"), A.mult)
    cnt = V2("Pc", 63, 512, 64)
    mm(V2("b4", 16, 24), V2("Tri"), cnt, True, True)
    f2 = V2("b5", 0, 64)
    mm(f2, V2("Id192"), V2("ownb"), True, False)
    for s in range(N):
        mm(f2, IdM, V2("Dc", 64 * s, 64 * s + 64), False, False)
    for s in range(N):
        ts(V2("Of", 64 * s, 64 * s + 64), V2("ownb"), float(owner[s]), V2("b4", 16 + s, 17 + s), A.is_equal, A.mult)
        mm(f2, IdM, V2("Of", 64 * s, 64 * s + 64), False, s == N - 1)
    ts(V2("ot"), V2("b4", 16, 24), -2.0, 1.0, A.mult, A.add)
    cp((T.rnS[:, :, 1], [("rnS", 2 * s + 1, 2 * s + 2) for s in range(N)]), cnt)
    ts(V2("F2u"), f2, -1.0, None, A.add)
    tt((T.rnS[:, :, 0], [("rnS", 2 * s, 2 * s + 1) for s in range(N)]), V2("ot"), cnt, A.subtract)
    send([(s, owner[s], V3("rnS", s, s + 1, 0, 2), T.rn[:, s, :]) for s in FAR], "rn")
    aff(V2("Za"), V2("Zs"), [[-16, 9], [0, 16]], A.is_ge, 0, 1)
    aff(V2("Zt"), V2("Za"), [[16, 9], [0, 16]], A.is_ge, 2, -1)
    aff(V2("Zs"), V2("Za"), [[16, 9], [0, 16]], A.is_ge, 15, -1)
    iota(V2("Ci"), [[0, 3], [2048, 3], [0, LC]], 0, 0, True)
    aff(V2("Zb"), V2("Zs"), [[-16, 9], [0, 16]], A.is_ge, -3, 1)
    aff(V2("Zi"), V2("Zb"), [[16, 9], [0, 16]], A.is_ge, 4, -1)

    vxs = (T.VxS[:], [("VxS%d" % u, u, 1024) for u in range(16)])
    cp(IX(V2("Vwin"), V2("F2u")), vxs)
    for s in range(N):
        q = owner[s]
        dma("ys"[s % 2], V3("vl", s, s + 1, 0, LC), (T.Vwin[0:128:16, CAPQ * q:CAPQ * q + CAPQ], [("Vwin", CAPQ * q, CAPQ * q + CAPQ)]))

    def piece(j):
        dma("y", (T.W1[j:128:16, :], [("W1p%d" % j, 0, 2048)]), V2("p%d" % j), [("W1", 0, 2048)])

    def pieces():
        piece(4)
        ts(V2("T0"), V2("thrI"), 4096.0, None, A.mult)
        tt(V2("T1"), V2("T0"), V2("aliI"), A.add)
        ts(V2("T2"), V2("T1"), 16777216.0, None, A.min)
        cp(V2("p0"), V2("T2"))
        tt(V2("r1"), V2("T2"), V2("p0"), A.subtract)
        cp(V2("p1"), V2("r1"))
        tt(V2("p2"), V2("r1"), V2("p1"), A.subtract)
        for j in range(3):
            piece(j)
    tab = (T.W1[:], [("W1", 0, 2048)] + [("W1p%d" % j, 0, 2048) for j in (0, 1, 2, 4)])

    def RN(s, k):
        return V3("rnS" if s == S0 else "rn", s, s + 1, k, k + 1)

    for s in range(N):
        act(V2("ab", CAPQ * s, CAPQ * s + CAPQ), V2("jc"), F.Abs, bias=RN(s, 0))

    def masks(a, b):
        for s in range(a, b):
            ts(V2("mk", CAPQ * s, CAPQ * s + CAPQ), V2("ab", CAPQ * s, CAPQ * s + CAPQ), RN(s, 1), float(2 ** (20 - asker[s])), A.is_lt, A.mult)

    def ylist():
        ts(V2("F2i"), f2, -1.0, None, A.add)
        ts(V2("own176"), V2("ownb"), 176.0, None, A.mult)
        ts(V2("own2k"), V2("ownb"), 2048.0, None, A.mult)
        ts(V2("ya"), V2("F2i"), 10923.0, None, A.mult)
        ts(V2("yc"), V2("F2i"), 16.0, None, A.mult)
        ts(V2("yb"), V2("ya"), 17, None, A.arith_shift_right)
        tt(V2("yc"), V2("yc"), V2("own176"), A.add)
        ts(V2("yb"), V2("yb"), -191.0, None, A.mult)
        tt(V2("yd"), V2("yb"), V2("yc"), A.add)
        cp(V2("yo"), V2("yd"))

    def hashes(c):
        a, b = HS[c]

        def W(nm):
            return V3(nm, a, b, 0, 48)

        def out(sem, src, dst):
            for gr in GRP:
                if a <= gr[0] < b:
                    send([(s, owner[s], src(s), dst(s)) for s in gr], sem)
        e = b if c == 0 else N
        for i in range(4 if c < 2 else 0):
            kk = ((1597 * (i + 1)) & 4095) - 4096
            ts(V3("hx", a, e, LC * i, LC * i + LC), V3("vl", a, e, 0, LC), 4096.0 * kk + 2048.0 * 4097.0, None, A.add)
        ts(W("hL"), W("hx"), 12, 4095, A.arith_shift_right, A.bitwise_and)
        ts(W("h4"), W("hx"), 4095, None, A.bitwise_and)
        tt(W("hq"), W("hL"), W("hL"), A.mult)
        p = V2("b6", 48 * a, 48 * b)
        ts(p, W("h4"), 64.0, -262144.0, A.mult, A.add)
        tt(W("ht"), W("hq"), p, A.add)
        ts(p, W("hL"), 64.0, -262144.0, A.mult, A.add)
        ts(W("hB"), W("ht"), 6, 4095, A.arith_shift_right, A.bitwise_and)
        tt(W("hb"), W("hB"), W("hB"), A.mult)
        tt(W("hu"), W("hb"), p, A.add)
        ts(p, W("hB"), 4096.0, 2048.0, A.mult, A.add)
        ts(W("he"), W("hu"), 7, 2047, A.arith_shift_right, A.bitwise_and)
        cp(V2("le", 48 * a, 48 * b), W("he"))
        out("rl", lambda s: V2("le", 48 * s, 48 * s + 48), lambda s: T.rl[:, 48 * s:48 * s + 48])
        tt(W("msg"), W("he"), p, A.add)
        out("rq", lambda s: V3("msg", s, s + 1, 0, 48), lambda s: T.rq[:, s, :])

    def look(c):
        a, b = CH[c]
        lst = "le" if a == S0 else "rl"
        for s in range(a, b):
            act(V2("GT", 768 * s, 768 * s + 768), IX(tab, V2(lst, 48 * s, 48 * s + 48)))

    def arrive(c):
        a, b = CH[c]
        for i in range(16):
            mm(V2(TB[c % 3], 0, 48 * (b - a)), Z("Zt", i), V2("GT", 768 * a + i, 768 * b, 16), i == 0, i == 15)

    def filt(c):
        a, b = CH[c]
        tt(V3("mn", a, b, 0, 48), V3("msg" if a == S0 else "rq", a, b, 0, 48), V2(TB[c % 3], 0, 48 * (b - a)), A.min)
        ts(V3("cI", a, b, 0, 48), V3("mn", a, b, 0, 48), 2047, None, A.bitwise_and)
        cp(V2("ls", 36 * a, 36 * b), V3("cI", a, b, 0, 36))
        for s in range(a, b):
            for i in range(3):
                o = 576 * s + CAPQ * i
                tt(V2("MG", o, o + CAPQ), IX(V2("seenS"), V2("ls", 36 * s + LC * i, 36 * s + LC * i + LC)), V2("mk", CAPQ * s, CAPQ * s + CAPQ), A.mult)
        o = V2("b%d" % (2 + c % 2), 0, 36 * (b - a))
        mm(o, IdM, V2("Ci", 0, 36 * (b - a)), True, False)
        for i in range(16):
            mm(o, Z("Zs", i), V2("MG", 576 * a + i, 576 * b, 16), False, i == 15)
        ts(V3("ky", a, b, 36, 48), V3("cI", a, b, 36, 48), 6144.0, None, A.add)

    def pick(c):
        a, b = CH[c]
        cp(V2("sI", 36 * a, 36 * b), V2("b%d" % (2 + c % 2), 0, 36 * (b - a)))
        ts(V3("sb", a, b, 0, 36), V2("sI", 36 * a, 36 * b), 2 ** 20 + 3 * 2048, None, A.bitwise_and)
        tt(V3("ky", a, b, 0, 36), V3("sb", a, b, 0, 36), V3("cI", a, b, 0, 36), A.add)
        tt(V3("m2", a, b, 0, 24), V3("ky", a, b, 0, 24), V3("ky", a, b, 24, 48), A.min)
        x = (LC * a, LC * b)
        tt(V2("kc", *x), V3("m2", a, b, 0, 12), V3("m2", a, b, 12, 24), A.min)
        ts(V2("xI", *x), V2("kc", *x), 2047, None, A.bitwise_and)
        cp(V2("lx", *x), V2("xI", *x))
        if a == S0:
            act(V2("land", CAPQ * me, CAPQ * me + CAPQ), IX(V2("vecS"), V2("lx", *x)))
            return
        act(V2("rs", CAPQ * a, CAPQ * b), IX(V2("vecS"), V2("lx", *x)))
        for gr in GRP:
            if a <= gr[0] < b:
                send([(s, asker[s], V2("lx", LC * s, LC * s + LC), T.lr[:, LC * s:LC * s + LC]) for s in gr], "lr")
                send([(s, asker[s], V2("rs", CAPQ * s, CAPQ * s + CAPQ), T.land[:, CAPQ * me:CAPQ * me + CAPQ]) for s in gr], "la")

    def items(c):
        for s in range(*CH[c]):
            o = CAPQ * owner[s]
            act(V2("IDx", o, o + CAPQ), IX(tab, V2("lx" if s == S0 else "lr", LC * s, LC * s + LC)))

    BLOCK = {"H": hashes, "G": look, "A": arrive, "F": filt, "P": pick, "I": items, "Y": ylist, "M": masks, "T": pieces}
    for blocks in PLAN:
        turns = []
        for n, (k, f, *y) in enumerate(blocks):
            stream[0] = []
            BLOCK[f](*y)
            started = False
            for (q, h) in stream[0]:
                k += 1 if q == "v" and started else 0
                started = True
                turns.append((k, n, len(turns), h))
        stream[0] = None
        for x in sorted(turns, key=lambda x: x[:3]):
            x[3]()

    def ygat(h):
        return V2("yS", 512 * h, 512 * h + 512), IX(V2("land"), V2("yo", 32 * h, 32 * h + 32))

    def igat(h):
        return V2("IDg", 512 * h, 512 * h + 512), IX(V2("IDx"), V2("yo", 32 * h, 32 * h + 32))
    act(*igat(1))
    cp(*igat(0))
    cp(*ygat(0))
    dma("y", hbm(T.y[:, 0:512]), V2("yS", 0, 512))
    act(*ygat(1))
    for i in range(16):
        mm(V2("b4", 64, 128), Z("Zi", i), V2("IDg", i, 1024, 16), i == 0, i == 15)
    tt(V2("chS"), V2("own2k"), V2("b4", 64, 128), A.add)
    dma("s", hbm(T.y[:, 512:1024]), V2("yS", 512, 1024))
    dma("s", hbm(T.chosen[:]), V2("chS"))

    for s, n in count.items():
        if clock["g"].get(s, 0) < n:
            g.wait_ge(T.sem[s], n)
